import numpy as np
import ml_dtypes


def mxq(x, axis, fmt="e4m3"):
    dtype, down = {"e4m3": (ml_dtypes.float8_e4m3fn, 7), "e5m2": (ml_dtypes.float8_e5m2, 14)}[fmt]
    v = np.moveaxis(np.asarray(x, np.float32).astype(ml_dtypes.bfloat16).astype(np.float64), axis, -1)
    blocks = v.reshape(v.shape[:-1] + (-1, 32))
    amax = np.abs(blocks).max(-1, keepdims=True)
    byte = np.maximum(np.where(amax > 0, np.frexp(amax)[1] - 1 + 127, 0) - down, 1)
    scale = np.exp2(byte - 127.0)
    codes = (blocks / scale).astype(np.float32).astype(dtype).astype(np.float64)
    return np.moveaxis((codes * scale).reshape(v.shape), -1, axis)


WIDE = False


def mx_kscale(k):
    if not WIDE:
        return np.ones(k)
    levels = np.array([10, -10, 5, -5, 0])
    if k % 512:
        return np.exp2(np.random.permutation(np.resize(levels, k // 32))).repeat(32)
    a = np.empty((k // 512, 16))
    for p in range(k // 512):
        a[p, :8] = np.random.permutation(np.resize(levels, 8))
        for g in range(8):
            far = levels[np.abs(levels - a[p, g]) >= 10]
            a[p, g + 8] = far[np.random.randint(len(far))]
    return np.exp2(a.ravel()).repeat(32)


def f64(x):
    return np.asarray(x).astype(np.float64)


def striped(idx):
    return np.tile(idx.reshape(-1, 16).T, (8, 1)).astype(np.uint16)


def unstriped(offs):
    return offs[:16].T.reshape(-1).astype(np.int64)


E2M1 = np.array([0.0, 0.5, 1.0, 1.5, 2.0, 3.0, 4.0, 6.0, -0.0, -0.5, -1.0, -1.5, -2.0, -3.0, -4.0, -6.0])


def pack_weight(w, fmt):
    k, n = w.shape
    w = f64(np.asarray(w, np.float32).astype(ml_dtypes.bfloat16)).reshape(k // 32, 32, n)
    amax = np.abs(w).max(1)
    if fmt == "e4m3":
        byte = np.frexp(amax)[1] - 1 + 127 - 7
    else:
        mant, ex = np.frexp(amax / 6.0)
        byte = np.where(mant > 0.5, ex, ex - 1) + 127
    byte = np.clip(np.where(amax > 0, byte, 1), 1, 254)
    scaled = (w * np.exp2(127.0 - byte)[:, None, :]).reshape(k, n).astype(np.float32)
    by_word = np.ascontiguousarray(scaled.reshape(k // 512, 128, 4, n).transpose(0, 1, 3, 2))
    if fmt == "e4m3":
        words = by_word.astype(ml_dtypes.float8_e4m3fn).view(np.uint8)
    else:
        c = by_word.astype(ml_dtypes.float4_e2m1fn).view(np.uint8) & 0xF
        words = (c[..., 0::2] | (c[..., 1::2] << 4)).reshape(k // 512, 128, 2 * n)
    return np.ascontiguousarray(words), np.ascontiguousarray(byte.astype(np.uint8).reshape(k // 512, 16, n))


def unpack_weight(words, scales, fmt):
    g, _, n = scales.shape
    words = np.ascontiguousarray(words).reshape(g, 128, n, -1)
    if fmt == "e4m3":
        vals = words.view(ml_dtypes.float8_e4m3fn).astype(np.float64)
    else:
        nib = np.empty((g, 128, n, 4), np.uint8)
        nib[..., 0::2] = words & 0xF
        nib[..., 1::2] = words >> 4
        vals = E2M1[nib]
    vals = vals * np.repeat(np.exp2(scales.astype(np.float64) - 127.0), 8, axis=1)[..., None]
    return vals.transpose(0, 1, 3, 2).reshape(g * 512, n)


def gelu(v):
    return 0.5 * v * (1.0 + np.tanh(np.sqrt(2.0 / np.pi) * (v + 0.044715 * v**3)))


def striped8(idx):
    return np.concatenate([v.reshape(-1, 16).T for v in idx]).astype(np.uint16)


def unstriped8(offs):
    return np.stack([offs[16 * g:16 * g + 16].T.reshape(-1) for g in range(8)]).astype(np.int64)


def heads(xT, wgt, idx8):
    k = np.arange(xT.shape[0])
    return wgt[k // 4 % 128] * xT[k[:, None], idx8[k % 512 // 64]]


K, T, S, H, N, G, R = 1024, 2048, 1024, 1024, 512, 8, 16

def setup_inputs():
    n = np.random.standard_normal
    s = mx_kscale(K)[:, None]
    u = mx_kscale(H)[:, None]
    xT = n((K, T)) * s
    idx8 = np.stack([np.random.permutation(T)[:S] for _ in range(G)])
    wgt = np.repeat(np.random.uniform(0.5, 2.0, (G, S)), R, axis=0)
    w1 = n((K, H)) / np.sqrt(K) / s * u.T
    b1 = 0.5 * n(H) * u[:, 0]
    wa_words, wa_scales = pack_weight(n((H, N)) / np.sqrt(H) / u, "e2m1")
    wb = 0.5 * n((H, N)) / np.sqrt(H) / (u * u)
    return {"xT": xT.astype(np.float32), "wgt": wgt.astype(np.float32),
            "offs": striped8(idx8),
            "w1": w1.astype(np.float32), "b1": b1.astype(np.float32),
            "wa_words": wa_words, "wa_scales": wa_scales,
            "wb": wb.astype(np.float32),
            "drive": n((N, S)).astype(np.float32)}

def reference(xT, wgt, offs, w1, b1, wa_words, wa_scales, wb, drive):
    xg = heads(f64(xT), f64(wgt), unstriped8(offs))
    xq = mxq(xg, 0, "e4m3")
    w1q = mxq(f64(w1), 0, "e4m3")
    z = (w1q.T @ xq) + f64(b1)[:, None]
    zq = mxq(z, 0, "e4m3")
    sq = mxq(z * z, 0, "e4m3")
    wa = unpack_weight(wa_words, wa_scales, "e2m1")
    wbq = mxq(f64(wb), 0, "e4m3")
    y = wa.T @ zq + wbq.T @ sq
    return y + f64(drive)

@@ -1,0 +1,240 @@
+from contextlib import ExitStack
+
+import concourse.mybir as mybir
+
+K, T, S, H, N = 1024, 2048, 1024, 1024, 512
+FLOPS = 2 * K * H * S + 2 * 2 * H * N * S
+
+F32 = mybir.dt.float32
+BF16 = mybir.dt.bfloat16
+I32 = mybir.dt.int32
+U32 = mybir.dt.uint32
+U16 = mybir.dt.uint16
+U8 = mybir.dt.uint8
+FP8X4 = mybir.dt.float8_e4m3fn_x4
+FP4X4 = mybir.dt.float4_e2m1fn_x4
+MULT = mybir.AluOpType.mult
+ADD = mybir.AluOpType.add
+IDENTITY = mybir.ActivationFunctionType.Identity
+SQUARE = mybir.ActivationFunctionType.Square
+
+P = 128
+PACK = 4
+KP = P * PACK
+W = 512
+
+
+def tile_list_koopman_delay_lift_kernel(tc, xT, wgt, offs, w1, b1, wa_words, wa_scales, wb, drive, out):
+    nc = tc.nc
+    with ExitStack() as ctx:
+        keep = ctx.enter_context(tc.tile_pool(name="keep", bufs=1))
+        raw = ctx.enter_context(tc.tile_pool(name="raw", bufs=6))
+        planes4 = ctx.enter_context(tc.tile_pool(name="planes4", bufs=4))
+        woven = ctx.enter_context(tc.tile_pool(name="woven", bufs=6))
+        zbank = ctx.enter_context(tc.psum_pool(name="zbank", bufs=4))
+        ybank = ctx.enter_context(tc.psum_pool(name="ybank", bufs=4))
+
+        offsets = keep.tile([P, S // 16], U16, name="offsets")
+        nc.sync.dma_start(offsets[:], offs)
+
+        wa_plane = keep.tile([P, 2, N], U8, name="wa_plane", align_bytes=64)
+        nc.gpsimd.memset(wa_plane[:].bitcast(I32), 0)
+        bias = keep.tile([P, 2, PACK], F32, name="bias")
+        nc.gpsimd.dma_start(out=bias[:], in_=b1.rearrange("(b p t) -> p b t", b=2, t=PACK))
+        for q in range(4):
+            nc.gpsimd.dma_start(
+                out=wa_plane[32 * q : 32 * q + 4].bitcast(I32),
+                in_=wa_scales[:, 4 * q : 4 * q + 4, :].rearrange("a r c -> r a c").bitcast(I32),
+            )
+
+        x_rows = xT.rearrange("(a p i) t -> a i p t", a=2, i=PACK)
+        x_plane = {}
+        weight = {}
+
+        def load_x(a, i):
+            x_plane[a, i] = keep.tile([P, T], F32, name="x_%d_%d" % (a, i))
+            nc.sync.dma_start(out=x_plane[a, i][:], in_=x_rows[a, i])
+
+        def load_rows(src):
+            t = raw.tile([P, PACK, W], F32, name="raw_rows")
+            nc.sync.dma_start(out=t[:], in_=src)
+            return t
+
+        load_x(0, 0)
+        for h in range(2):
+            weight[h] = keep.tile([P, W], F32, name="wgt_%d" % h)
+            nc.sync.dma_start(out=weight[h][:], in_=wgt[:, h * W : (h + 1) * W])
+        w1_rows = w1.rearrange("(a p j) r -> a p j r", a=2, j=PACK)
+        w1_raw = {}
+        for a, i in ((0, 1), (0, 2), (0, 3), (1, 0), (1, 1)):
+            load_x(a, i)
+        w1_raw[0, 0] = load_rows(w1_rows[0][:, :, 0:W])
+        load_x(1, 2)
+        load_x(1, 3)
+        for a, b in ((1, 0), (0, 1), (1, 1)):
+            w1_raw[a, b] = load_rows(w1_rows[a][:, :, b * W : (b + 1) * W])
+        wb_rows = wb.rearrange("(b p j) n -> b p j n", b=2, j=PACK)
+        wb_raw = {}
+        wb_raw[0] = load_rows(wb_rows[0])
+        wa_codes = keep.tile([P, 2, 2 * N], U8, name="wa_codes", align_bytes=64)
+        nc.sync.dma_start(out=wa_codes[:].bitcast(I32), in_=wa_words.rearrange("a p c -> p a c").bitcast(I32))
+        wb_raw[1] = load_rows(wb_rows[1])
+        drive_rows = drive.rearrange("(g p) j -> p g j", p=P)
+        out_rows = out.rearrange("(g p) j -> p g j", p=P)
+        result = {}
+        for h in range(2):
+            result[h] = load_rows(drive_rows[:, :, h * W : (h + 1) * W])
+
+        def weave_views(src):
+            dst = woven.tile([P, W, PACK], BF16, name="woven_rows", align_bytes=64)
+            return (dst, dst[:].rearrange("p (c i) t -> p c t i", i=4), src[:].rearrange("p t (c i) -> p c t i", i=4))
+
+        def weave(engine, src):
+            dst, o, i = weave_views(src)
+            if engine == "v":
+                nc.vector.tensor_copy(out=o, in_=i)
+            else:
+                nc.scalar.copy(out=o, in_=i)
+            return dst
+
+        def weave_w1(engine, src):
+            dst = woven.tile([P, W, PACK], BF16, name="woven_rows", align_bytes=64)
+            o = dst[:].rearrange("p (t m) j -> p m j t", t=PACK)
+            i = src[:].rearrange("p j (m t) -> p m j t", t=PACK)
+            if engine == "v":
+                nc.vector.tensor_copy(out=o, in_=i)
+            else:
+                nc.scalar.copy(out=o, in_=i)
+            return dst
+
+        def quantise(src, name):
+            codes = keep.tile([P, W], U32, name=name + "_codes", align_bytes=64)
+            scales = keep.tile([P, W], U8, name=name + "_scales", align_bytes=64)
+            nc.vector.quantize_mx(out=codes[:].bitcast(FP8X4), scales=scales[:], in_=src[:].rearrange("p w j -> p (w j)"))
+            return codes, scales
+
+        picked = {}
+
+        def gather(a, i):
+            for h in range(2):
+                if i == 0:
+                    picked[a, h] = planes4.tile([P, PACK, W], F32, name="planes")
+                nc.vector.tensor_tensor(
+                    picked[a, h][:, i, :],
+                    x_plane[a, i][:].indirect(offsets[:, h * (W // 16) : (h + 1) * (W // 16)]),
+                    weight[h][:],
+                    MULT,
+                )
+
+        xq, w1q, wbq, zq, sq = {}, {}, {}, {}, {}
+        xw = {}
+        for i in range(PACK):
+            gather(0, i)
+        for h in range(2):
+            xw[0, h] = weave("s", picked[0, h])
+        gather(1, 0)
+        gather(1, 1)
+        xq[0, 0] = quantise(xw[0, 0], "xq00")
+        xq[0, 1] = quantise(xw[0, 1], "xq01")
+        w00 = weave_w1("s", w1_raw[0, 0])
+        gather(1, 2)
+        w1q[0, 0] = quantise(w00, "w1q00")
+        gather(1, 3)
+        for h in range(2):
+            xw[1, h] = weave("s", picked[1, h])
+        w10 = weave_w1("v", w1_raw[1, 0])
+        xq[1, 0] = quantise(xw[1, 0], "xq10")
+        w1q[1, 0] = quantise(w10, "w1q10")
+        xq[1, 1] = quantise(xw[1, 1], "xq11")
+
+        def lift(b, h, pass_major):
+            banks = [zbank.tile([P, W], F32, name="zb") for t in range(PACK)]
+            order = [(t, a) for t in range(PACK) for a in range(2)]
+            if pass_major:
+                order = [(t, a) for a in range(2) for t in range(PACK)]
+            z32 = planes4.tile([P, PACK, W], F32, name="planes")
+            for t, a in order:
+                cols = slice(t * P, (t + 1) * P)
+                nc.tensor.matmul_mx(
+                    out=banks[t][:],
+                    lhsT=w1q[a, b][0][:, cols].bitcast(FP8X4),
+                    lhsT_scale=w1q[a, b][1][:, cols],
+                    rhs=xq[a, h][0][:].bitcast(FP8X4),
+                    rhs_scale=xq[a, h][1][:],
+                    start=(a == 0),
+                    stop=(a == 1),
+                )
+                if a == 1:
+                    nc.scalar.activation(out=z32[:, t, :], in_=banks[t][:], func=IDENTITY, bias=bias[:, b, t : t + 1])
+            return z32
+
+        def square(z32):
+            dst, o, i = weave_views(z32)
+            nc.scalar.activation(out=o, in_=i, func=SQUARE)
+            return dst
+
+        ybanks = {}
+
+        def predict(b, h, kind):
+            if h not in ybanks:
+                ybanks[h] = [ybank.tile([P, W], F32, name="yb") for g in range(4)]
+            for g in range(4):
+                cols = slice(g * P, (g + 1) * P)
+                if kind == "z":
+                    lhs = wa_codes[:, b, 2 * g * P : 2 * (g + 1) * P].bitcast(FP4X4)
+                    lhs_scale = wa_plane[:, b, cols]
+                    rhs = zq[b, h]
+                else:
+                    lhs = wbq[b][0][:, cols].bitcast(FP8X4)
+                    lhs_scale = wbq[b][1][:, cols]
+                    rhs = sq[b, h]
+                last = b == 1 and kind == "s"
+                nc.tensor.matmul_mx(
+                    out=ybanks[h][g][:],
+                    lhsT=lhs,
+                    lhsT_scale=lhs_scale,
+                    rhs=rhs[0][:].bitcast(FP8X4),
+                    rhs_scale=rhs[1][:],
+                    start=(b == 0 and kind == "z"),
+                    stop=last,
+                )
+                if last:
+                    nc.vector.tensor_tensor(result[h][:, g, :], ybanks[h][g][:], result[h][:, g, :], ADD)
+                    nc.sync.dma_start(out=out_rows[:, g, h * W : (h + 1) * W], in_=result[h][:, g, :])
+
+        z = lift(0, 0, True)
+        s00 = square(z)
+        w01 = weave_w1("v", w1_raw[0, 1])
+        z00 = weave("v", z)
+        w1q[0, 1] = quantise(w01, "w1q01")
+        zq[0, 0] = quantise(z00, "zq00")
+        z = lift(0, 1, False)
+        w11 = weave_w1("v", w1_raw[1, 1])
+        sq[0, 0] = quantise(s00, "sq00")
+        w1q[1, 1] = quantise(w11, "w1q11")
+        s01 = square(z)
+        wb0 = weave("v", wb_raw[0])
+        z01 = weave("v", z)
+        wbq[0] = quantise(wb0, "wbq0")
+        zq[0, 1] = quantise(z01, "zq01")
+        z = lift(1, 0, False)
+        predict(0, 0, "z")
+        predict(0, 0, "s")
+        wb1 = weave("v", wb_raw[1])
+        sq[0, 1] = quantise(s01, "sq01")
+        wbq[1] = quantise(wb1, "wbq1")
+        s10 = square(z)
+        z10 = weave("v", z)
+        zq[1, 0] = quantise(z10, "zq10")
+        z = lift(1, 1, False)
+        sq[1, 0] = quantise(s10, "sq10")
+        predict(1, 0, "z")
+        s11 = square(z)
+        predict(1, 0, "s")
+        z11 = weave("v", z)
+        zq[1, 1] = quantise(z11, "zq11")
+        predict(0, 1, "z")
+        predict(0, 1, "s")
+        sq[1, 1] = quantise(s11, "sq11")
+        predict(1, 1, "z")
+        predict(1, 1, "s")

@@ -29,20 +29,19 @@ def tile_list_koopman_delay_lift_kernel(tc, xT, wgt, offs, w1, b1, wa_words, wa_
     with ExitStack() as ctx:
         keep = ctx.enter_context(tc.tile_pool(name="keep", bufs=1))
         raw = ctx.enter_context(tc.tile_pool(name="raw", bufs=6))
-        planes4 = ctx.enter_context(tc.tile_pool(name="planes4", bufs=4))
-        woven = ctx.enter_context(tc.tile_pool(name="woven", bufs=6))
-        zbank = ctx.enter_context(tc.psum_pool(name="zbank", bufs=4))
-        ybank = ctx.enter_context(tc.psum_pool(name="ybank", bufs=4))
+        planes4 = ctx.enter_context(tc.tile_pool(name="planes4", bufs=3))
+        woven = ctx.enter_context(tc.tile_pool(name="woven", bufs=4))
+        psum = ctx.enter_context(tc.psum_pool(name="psum", bufs=1))
 
         offsets = keep.tile([P, S // 16], U16, name="offsets")
         nc.sync.dma_start(offsets[:], offs)
 
         wa_plane = keep.tile([P, 2, N], U8, name="wa_plane", align_bytes=64)
-        nc.gpsimd.memset(wa_plane[:].bitcast(I32), 0)
+        nc.vector.memset(wa_plane[:].bitcast(I32), 0)
         bias = keep.tile([P, 2, PACK], F32, name="bias")
-        nc.gpsimd.dma_start(out=bias[:], in_=b1.rearrange("(b p t) -> p b t", b=2, t=PACK))
+        nc.scalar.dma_start(out=bias[:], in_=b1.rearrange("(b p t) -> p b t", b=2, t=PACK))
         for q in range(4):
-            nc.gpsimd.dma_start(
+            nc.scalar.dma_start(
                 out=wa_plane[32 * q : 32 * q + 4].bitcast(I32),
                 in_=wa_scales[:, 4 * q : 4 * q + 4, :].rearrange("a r c -> r a c").bitcast(I32),
             )
@@ -66,13 +65,12 @@ def tile_list_koopman_delay_lift_kernel(tc, xT, wgt, offs, w1, b1, wa_words, wa_
             nc.sync.dma_start(out=weight[h][:], in_=wgt[:, h * W : (h + 1) * W])
         w1_rows = w1.rearrange("(a p j) r -> a p j r", a=2, j=PACK)
         w1_raw = {}
-        for a, i in ((0, 1), (0, 2), (0, 3), (1, 0), (1, 1)):
+        for a, i in ((0, 1), (0, 2), (0, 3), (1, 0)):
             load_x(a, i)
-        w1_raw[0, 0] = load_rows(w1_rows[0][:, :, 0:W])
-        load_x(1, 2)
-        load_x(1, 3)
-        for a, b in ((1, 0), (0, 1), (1, 1)):
+        for i, (a, b) in enumerate(((0, 0), (1, 0), (0, 1))):
             w1_raw[a, b] = load_rows(w1_rows[a][:, :, b * W : (b + 1) * W])
+            load_x(1, i + 1)
+        w1_raw[1, 1] = load_rows(w1_rows[1][:, :, W : 2 * W])
         wb_rows = wb.rearrange("(b p j) n -> b p j n", b=2, j=PACK)
         wb_raw = {}
         wb_raw[0] = load_rows(wb_rows[0])
@@ -85,70 +83,85 @@ def tile_list_koopman_delay_lift_kernel(tc, xT, wgt, offs, w1, b1, wa_words, wa_
         for h in range(2):
             result[h] = load_rows(drive_rows[:, :, h * W : (h + 1) * W])
 
-        def weave_views(src):
-            dst = woven.tile([P, W, PACK], BF16, name="woven_rows", align_bytes=64)
-            return (dst, dst[:].rearrange("p (c i) t -> p c t i", i=4), src[:].rearrange("p t (c i) -> p c t i", i=4))
+        def woven_tile(ring):
+            if ring is None:
+                return woven.tile([P, W, PACK], BF16, name="woven_rows", align_bytes=64)
+            return keep.tile([P, W, PACK], BF16, name="ring_%d" % ring, align_bytes=64)
 
-        def weave(engine, src):
-            dst, o, i = weave_views(src)
+        def weave_views(dst, src, cols=slice(0, W)):
+            return (dst[:, cols, :].rearrange("p (c i) t -> p c t i", i=4), src[:, :, cols].rearrange("p t (c i) -> p c t i", i=4))
+
+        def copy_on(engine, o, i):
             if engine == "v":
                 nc.vector.tensor_copy(out=o, in_=i)
             else:
                 nc.scalar.copy(out=o, in_=i)
+
+        def weave(engine, src, ring=None):
+            dst = woven_tile(ring)
+            copy_on(engine, *weave_views(dst, src))
             return dst
 
-        def weave_w1(engine, src):
-            dst = woven.tile([P, W, PACK], BF16, name="woven_rows", align_bytes=64)
-            o = dst[:].rearrange("p (t m) j -> p m j t", t=PACK)
-            i = src[:].rearrange("p j (m t) -> p m j t", t=PACK)
-            if engine == "v":
-                nc.vector.tensor_copy(out=o, in_=i)
-            else:
-                nc.scalar.copy(out=o, in_=i)
+        def weave_w1(engine, src, ring=None):
+            dst = woven_tile(ring)
+            copy_on(engine, dst[:].rearrange("p (t m) j -> p m j t", t=PACK), src[:].rearrange("p j (m t) -> p m j t", t=PACK))
             return dst
 
-        def quantise(src, name):
-            codes = keep.tile([P, W], U32, name=name + "_codes", align_bytes=64)
+        def quantise(src, name, codes_name=None):
+            codes = keep.tile([P, W], U32, name=codes_name or name + "_codes", align_bytes=64)
             scales = keep.tile([P, W], U8, name=name + "_scales", align_bytes=64)
             nc.vector.quantize_mx(out=codes[:].bitcast(FP8X4), scales=scales[:], in_=src[:].rearrange("p w j -> p (w j)"))
             return codes, scales
 
         picked = {}
 
-        def gather(a, i):
-            for h in range(2):
-                if i == 0:
-                    picked[a, h] = planes4.tile([P, PACK, W], F32, name="planes")
-                nc.vector.tensor_tensor(
-                    picked[a, h][:, i, :],
-                    x_plane[a, i][:].indirect(offsets[:, h * (W // 16) : (h + 1) * (W // 16)]),
-                    weight[h][:],
-                    MULT,
-                )
+        def gather(a, i, h):
+            if i == 0 and (a, h) == (1, 0):
+                picked[a, h] = keep.tile([P, PACK, W], F32, name="picked_last", align_bytes=64)
+            elif i == 0:
+                picked[a, h] = planes4.tile([P, PACK, W], F32, name="planes")
+            nc.vector.tensor_tensor(
+                picked[a, h][:, i, :],
+                x_plane[a, i][:].indirect(offsets[:, h * (W // 16) : (h + 1) * (W // 16)]),
+                weight[h][:],
+                MULT,
+            )
 
         xq, w1q, wbq, zq, sq = {}, {}, {}, {}, {}
         xw = {}
         for i in range(PACK):
-            gather(0, i)
+            for h in range(2):
+                gather(0, i, h)
         for h in range(2):
             xw[0, h] = weave("s", picked[0, h])
-        gather(1, 0)
-        gather(1, 1)
-        xq[0, 0] = quantise(xw[0, 0], "xq00")
-        xq[0, 1] = quantise(xw[0, 1], "xq01")
         w00 = weave_w1("s", w1_raw[0, 0])
-        gather(1, 2)
+        w10 = weave_w1("s", w1_raw[1, 0])
+        w01 = weave_w1("s", w1_raw[0, 1], 1)
+        gather(1, 0, 0)
+        gather(1, 0, 1)
+        xq[0, 0] = quantise(xw[0, 0], "xq00")
+        gather(1, 1, 0)
+        gather(1, 1, 1)
+        xq[0, 1] = quantise(xw[0, 1], "xq01")
+        gather(1, 2, 0)
         w1q[0, 0] = quantise(w00, "w1q00")
-        gather(1, 3)
-        for h in range(2):
-            xw[1, h] = weave("s", picked[1, h])
-        w10 = weave_w1("v", w1_raw[1, 0])
-        xq[1, 0] = quantise(xw[1, 0], "xq10")
+        gather(1, 2, 1)
         w1q[1, 0] = quantise(w10, "w1q10")
+        gather(1, 3, 0)
+        xw[1, 0] = woven_tile(0)
+        copy_on("s", *weave_views(xw[1, 0], picked[1, 0], slice(0, W // 2)))
+        copy_on("v", *weave_views(xw[1, 0], picked[1, 0], slice(W // 2, W)))
+        gather(1, 3, 1)
+        xq[1, 0] = quantise(xw[1, 0], "xq10")
+        xw[1, 1] = weave("v", picked[1, 1], 0)
+        w1q[0, 1] = quantise(w01, "w1q01", "picked_last")
         xq[1, 1] = quantise(xw[1, 1], "xq11")
 
-        def lift(b, h, pass_major):
-            banks = [zbank.tile([P, W], F32, name="zb") for t in range(PACK)]
+        def four_banks(side):
+            return [psum.tile([P, W], F32, name="bank_%d" % (4 * side + t)) for t in range(4)]
+
+        def lift(b, h, side, pass_major):
+            banks = four_banks(side)
             order = [(t, a) for t in range(PACK) for a in range(2)]
             if pass_major:
                 order = [(t, a) for a in range(2) for t in range(PACK)]
@@ -169,7 +182,8 @@ def tile_list_koopman_delay_lift_kernel(tc, xT, wgt, offs, w1, b1, wa_words, wa_
             return z32
 
         def square(z32):
-            dst, o, i = weave_views(z32)
+            dst = woven_tile(None)
+            o, i = weave_views(dst, z32)
             nc.scalar.activation(out=o, in_=i, func=SQUARE)
             return dst
 
@@ -177,7 +191,7 @@ def tile_list_koopman_delay_lift_kernel(tc, xT, wgt, offs, w1, b1, wa_words, wa_
 
         def predict(b, h, kind):
             if h not in ybanks:
-                ybanks[h] = [ybank.tile([P, W], F32, name="yb") for g in range(4)]
+                ybanks[h] = four_banks(1 - h)
             for g in range(4):
                 cols = slice(g * P, (g + 1) * P)
                 if kind == "z":
@@ -188,7 +202,6 @@ def tile_list_koopman_delay_lift_kernel(tc, xT, wgt, offs, w1, b1, wa_words, wa_
                     lhs = wbq[b][0][:, cols].bitcast(FP8X4)
                     lhs_scale = wbq[b][1][:, cols]
                     rhs = sq[b, h]
-                last = b == 1 and kind == "s"
                 nc.tensor.matmul_mx(
                     out=ybanks[h][g][:],
                     lhsT=lhs,
@@ -196,45 +209,53 @@ def tile_list_koopman_delay_lift_kernel(tc, xT, wgt, offs, w1, b1, wa_words, wa_
                     rhs=rhs[0][:].bitcast(FP8X4),
                     rhs_scale=rhs[1][:],
                     start=(b == 0 and kind == "z"),
-                    stop=last,
+                    stop=(b == 1 and kind == "s"),
                 )
-                if last:
-                    nc.vector.tensor_tensor(result[h][:, g, :], ybanks[h][g][:], result[h][:, g, :], ADD)
-                    nc.sync.dma_start(out=out_rows[:, g, h * W : (h + 1) * W], in_=result[h][:, g, :])
 
-        z = lift(0, 0, True)
-        s00 = square(z)
-        w01 = weave_w1("v", w1_raw[0, 1])
-        z00 = weave("v", z)
-        w1q[0, 1] = quantise(w01, "w1q01")
-        zq[0, 0] = quantise(z00, "zq00")
-        z = lift(0, 1, False)
-        w11 = weave_w1("v", w1_raw[1, 1])
-        sq[0, 0] = quantise(s00, "sq00")
+        def finish(h, g):
+            nc.vector.tensor_tensor(result[h][:, g, :], ybanks[h][g][:], result[h][:, g, :], ADD)
+            nc.sync.dma_start(out=out_rows[:, g, h * W : (h + 1) * W], in_=result[h][:, g, :])
+
+        z00 = lift(0, 0, 0, True)
+        s00 = square(z00)
+        w11 = weave_w1("v", w1_raw[1, 1], 1)
+        wb0 = weave("v", wb_raw[0], 0)
         w1q[1, 1] = quantise(w11, "w1q11")
-        s01 = square(z)
-        wb0 = weave("v", wb_raw[0])
-        z01 = weave("v", z)
         wbq[0] = quantise(wb0, "wbq0")
-        zq[0, 1] = quantise(z01, "zq01")
-        z = lift(1, 0, False)
+
+        z01 = lift(0, 1, 1, False)
+        s01 = square(z01)
+        wb1 = weave("v", wb_raw[1], 1)
+        zw = weave("v", z00, 0)
+        wbq[1] = quantise(wb1, "wbq1")
+        zq[0, 0] = quantise(zw, "zq00")
+
+        z10 = lift(1, 0, 0, False)
+        s10 = square(z10)
+        zw = weave("v", z01, 1)
+        sq[0, 0] = quantise(s00, "sq00")
+        zq[0, 1] = quantise(zw, "zq01")
+        sq[0, 1] = quantise(s01, "sq01")
         predict(0, 0, "z")
         predict(0, 0, "s")
-        wb1 = weave("v", wb_raw[1])
-        sq[0, 1] = quantise(s01, "sq01")
-        wbq[1] = quantise(wb1, "wbq1")
-        s10 = square(z)
-        z10 = weave("v", z)
-        zq[1, 0] = quantise(z10, "zq10")
-        z = lift(1, 1, False)
+
+        z11 = lift(1, 1, 0, False)
+        s11 = square(z11)
+        zw = weave("v", z10, 0)
+        zq[1, 0] = quantise(zw, "zq10")
         sq[1, 0] = quantise(s10, "sq10")
         predict(1, 0, "z")
-        s11 = square(z)
         predict(1, 0, "s")
-        z11 = weave("v", z)
-        zq[1, 1] = quantise(z11, "zq11")
+        finish(0, 0)
+        finish(0, 1)
+        zw = weave("v", z11, 1)
+        finish(0, 2)
+        zq[1, 1] = quantise(zw, "zq11")
+        finish(0, 3)
         predict(0, 1, "z")
         predict(0, 1, "s")
-        sq[1, 1] = quantise(s11, "sq11")
         predict(1, 1, "z")
+        sq[1, 1] = quantise(s11, "sq11")
         predict(1, 1, "s")
+        for g in range(4):
+            finish(1, g)

@@ -28,8 +28,8 @@ def tile_list_koopman_delay_lift_kernel(tc, xT, wgt, offs, w1, b1, wa_words, wa_
     nc = tc.nc
     with ExitStack() as ctx:
         keep = ctx.enter_context(tc.tile_pool(name="keep", bufs=1))
-        raw = ctx.enter_context(tc.tile_pool(name="raw", bufs=6))
-        planes4 = ctx.enter_context(tc.tile_pool(name="planes4", bufs=3))
+        raw = ctx.enter_context(tc.tile_pool(name="raw", bufs=5))
+        planes4 = ctx.enter_context(tc.tile_pool(name="planes4", bufs=4))
         woven = ctx.enter_context(tc.tile_pool(name="woven", bufs=4))
         psum = ctx.enter_context(tc.psum_pool(name="psum", bufs=1))
 
@@ -38,13 +38,6 @@ def tile_list_koopman_delay_lift_kernel(tc, xT, wgt, offs, w1, b1, wa_words, wa_
 
         wa_plane = keep.tile([P, 2, N], U8, name="wa_plane", align_bytes=64)
         nc.vector.memset(wa_plane[:].bitcast(I32), 0)
-        bias = keep.tile([P, 2, PACK], F32, name="bias")
-        nc.scalar.dma_start(out=bias[:], in_=b1.rearrange("(b p t) -> p b t", b=2, t=PACK))
-        for q in range(4):
-            nc.scalar.dma_start(
-                out=wa_plane[32 * q : 32 * q + 4].bitcast(I32),
-                in_=wa_scales[:, 4 * q : 4 * q + 4, :].rearrange("a r c -> r a c").bitcast(I32),
-            )
 
         x_rows = xT.rearrange("(a p i) t -> a i p t", a=2, i=PACK)
         x_plane = {}
@@ -65,12 +58,25 @@ def tile_list_koopman_delay_lift_kernel(tc, xT, wgt, offs, w1, b1, wa_words, wa_
             nc.sync.dma_start(out=weight[h][:], in_=wgt[:, h * W : (h + 1) * W])
         w1_rows = w1.rearrange("(a p j) r -> a p j r", a=2, j=PACK)
         w1_raw = {}
-        for a, i in ((0, 1), (0, 2), (0, 3), (1, 0)):
+        for a, i in ((0, 1), (0, 2), (0, 3), (1, 0), (1, 1)):
             load_x(a, i)
-        for i, (a, b) in enumerate(((0, 0), (1, 0), (0, 1))):
-            w1_raw[a, b] = load_rows(w1_rows[a][:, :, b * W : (b + 1) * W])
-            load_x(1, i + 1)
-        w1_raw[1, 1] = load_rows(w1_rows[1][:, :, W : 2 * W])
+        w1_raw[0, 0] = load_rows(w1_rows[0][:, :, 0:W])
+        bias = keep.tile([P, 2, PACK], F32, name="bias")
+        nc.sync.dma_start(out=bias[:], in_=b1.rearrange("(b p t) -> p b t", b=2, t=PACK))
+        load_x(1, 2)
+        load_x(1, 3)
+        w10_half = []
+        for u in range(2):
+            half = keep.tile([P, PACK, W // 2], F32, name="w10_half_%d" % u, align_bytes=64)
+            nc.sync.dma_start(out=half[:], in_=w1_rows[1][:, :, u * (W // 2) : (u + 1) * (W // 2)])
+            w10_half.append(half)
+        for a in range(2):
+            w1_raw[a, 1] = load_rows(w1_rows[a][:, :, W : 2 * W])
+        for q in range(4):
+            nc.sync.dma_start(
+                out=wa_plane[32 * q : 32 * q + 4].bitcast(I32),
+                in_=wa_scales[:, 4 * q : 4 * q + 4, :].rearrange("a r c -> r a c").bitcast(I32),
+            )
         wb_rows = wb.rearrange("(b p j) n -> b p j n", b=2, j=PACK)
         wb_raw = {}
         wb_raw[0] = load_rows(wb_rows[0])
@@ -116,9 +122,7 @@ def tile_list_koopman_delay_lift_kernel(tc, xT, wgt, offs, w1, b1, wa_words, wa_
         picked = {}
 
         def gather(a, i, h):
-            if i == 0 and (a, h) == (1, 0):
-                picked[a, h] = keep.tile([P, PACK, W], F32, name="picked_last", align_bytes=64)
-            elif i == 0:
+            if i == 0:
                 picked[a, h] = planes4.tile([P, PACK, W], F32, name="planes")
             nc.vector.tensor_tensor(
                 picked[a, h][:, i, :],
@@ -135,8 +139,6 @@ def tile_list_koopman_delay_lift_kernel(tc, xT, wgt, offs, w1, b1, wa_words, wa_
         for h in range(2):
             xw[0, h] = weave("s", picked[0, h])
         w00 = weave_w1("s", w1_raw[0, 0])
-        w10 = weave_w1("s", w1_raw[1, 0])
-        w01 = weave_w1("s", w1_raw[0, 1], 1)
         gather(1, 0, 0)
         gather(1, 0, 1)
         xq[0, 0] = quantise(xw[0, 0], "xq00")
@@ -144,18 +146,24 @@ def tile_list_koopman_delay_lift_kernel(tc, xT, wgt, offs, w1, b1, wa_words, wa_
         gather(1, 1, 1)
         xq[0, 1] = quantise(xw[0, 1], "xq01")
         gather(1, 2, 0)
-        w1q[0, 0] = quantise(w00, "w1q00")
         gather(1, 2, 1)
-        w1q[1, 0] = quantise(w10, "w1q10")
+        w1q[0, 0] = quantise(w00, "w1q00")
         gather(1, 3, 0)
         xw[1, 0] = woven_tile(0)
         copy_on("s", *weave_views(xw[1, 0], picked[1, 0], slice(0, W // 2)))
         copy_on("v", *weave_views(xw[1, 0], picked[1, 0], slice(W // 2, W)))
         gather(1, 3, 1)
         xq[1, 0] = quantise(xw[1, 0], "xq10")
-        xw[1, 1] = weave("v", picked[1, 1], 0)
-        w1q[0, 1] = quantise(w01, "w1q01", "picked_last")
-        xq[1, 1] = quantise(xw[1, 1], "xq11")
+        w10 = woven_tile(1)
+        for u, engine in enumerate("sv"):
+            copy_on(
+                engine,
+                w10[:].rearrange("p (t m) j -> p m j t", t=PACK)[:, u * (P // 2) : (u + 1) * (P // 2)],
+                w10_half[u][:].rearrange("p j (m t) -> p m j t", t=PACK),
+            )
+        w1q[1, 0] = quantise(w10, "w1q10")
+        xw[1, 1] = keep.tile([P, W, PACK], BF16, name="w10_half_0", align_bytes=64)
+        copy_on("s", *weave_views(xw[1, 1], picked[1, 1]))
 
         def four_banks(side):
             return [psum.tile([P, W], F32, name="bank_%d" % (4 * side + t)) for t in range(4)]
@@ -218,31 +226,34 @@ def tile_list_koopman_delay_lift_kernel(tc, xT, wgt, offs, w1, b1, wa_words, wa_
 
         z00 = lift(0, 0, 0, True)
         s00 = square(z00)
+        w01 = weave_w1("v", w1_raw[0, 1], 0)
+        xq[1, 1] = quantise(xw[1, 1], "xq11")
+        w1q[0, 1] = quantise(w01, "w1q01")
         w11 = weave_w1("v", w1_raw[1, 1], 1)
-        wb0 = weave("v", wb_raw[0], 0)
+        zw = weave("v", z00, 0)
         w1q[1, 1] = quantise(w11, "w1q11")
-        wbq[0] = quantise(wb0, "wbq0")
+        zq[0, 0] = quantise(zw, "zq00")
 
         z01 = lift(0, 1, 1, False)
         s01 = square(z01)
-        wb1 = weave("v", wb_raw[1], 1)
-        zw = weave("v", z00, 0)
-        wbq[1] = quantise(wb1, "wbq1")
-        zq[0, 0] = quantise(zw, "zq00")
+        wb0 = weave("v", wb_raw[0], 1)
+        sq[0, 0] = quantise(s00, "sq00")
+        zw = weave("v", z01, 0)
+        wbq[0] = quantise(wb0, "wbq0")
+        zq[0, 1] = quantise(zw, "zq01")
 
         z10 = lift(1, 0, 0, False)
         s10 = square(z10)
-        zw = weave("v", z01, 1)
-        sq[0, 0] = quantise(s00, "sq00")
-        zq[0, 1] = quantise(zw, "zq01")
-        sq[0, 1] = quantise(s01, "sq01")
         predict(0, 0, "z")
         predict(0, 0, "s")
+        wb1 = weave("v", wb_raw[1], 1)
+        sq[0, 1] = quantise(s01, "sq01")
+        zw = weave("v", z10, 0)
+        wbq[1] = quantise(wb1, "wbq1")
+        zq[1, 0] = quantise(zw, "zq10")
 
         z11 = lift(1, 1, 0, False)
         s11 = square(z11)
-        zw = weave("v", z10, 0)
-        zq[1, 0] = quantise(zw, "zq10")
         sq[1, 0] = quantise(s10, "sq10")
         predict(1, 0, "z")
         predict(1, 0, "s")

@@ -20,253 +20,242 @@ SQUARE = mybir.ActivationFunctionType.Square
 
 P = 128
 PACK = 4
-KP = P * PACK
+PASSES = 2
 W = 512
+GROUPS = N // P
+RUN = 4
+LIST_COLUMNS = W // 16
 
 
 def tile_list_koopman_delay_lift_kernel(tc, xT, wgt, offs, w1, b1, wa_words, wa_scales, wb, drive, out):
     nc = tc.nc
     with ExitStack() as ctx:
         keep = ctx.enter_context(tc.tile_pool(name="keep", bufs=1))
-        raw = ctx.enter_context(tc.tile_pool(name="raw", bufs=5))
-        planes4 = ctx.enter_context(tc.tile_pool(name="planes4", bufs=4))
+        loaded = ctx.enter_context(tc.tile_pool(name="loaded", bufs=5))
+        planes = ctx.enter_context(tc.tile_pool(name="planes", bufs=4))
         woven = ctx.enter_context(tc.tile_pool(name="woven", bufs=4))
         psum = ctx.enter_context(tc.psum_pool(name="psum", bufs=1))
 
         offsets = keep.tile([P, S // 16], U16, name="offsets")
         nc.sync.dma_start(offsets[:], offs)
 
-        wa_plane = keep.tile([P, 2, N], U8, name="wa_plane", align_bytes=64)
-        nc.vector.memset(wa_plane[:].bitcast(I32), 0)
+        wa_scale_rows = keep.tile([P, PASSES, N], U8, name="wa_scale_rows", align_bytes=64)
+        nc.vector.memset(wa_scale_rows[:].bitcast(I32), 0)
 
-        x_rows = xT.rearrange("(a p i) t -> a i p t", a=2, i=PACK)
+        x_rows = xT.rearrange("(a p i) t -> a i p t", a=PASSES, i=PACK)
         x_plane = {}
-        weight = {}
 
         def load_x(a, i):
             x_plane[a, i] = keep.tile([P, T], F32, name="x_%d_%d" % (a, i))
             nc.sync.dma_start(out=x_plane[a, i][:], in_=x_rows[a, i])
 
-        def load_rows(src):
-            t = raw.tile([P, PACK, W], F32, name="raw_rows")
-            nc.sync.dma_start(out=t[:], in_=src)
-            return t
+        def load_block(src):
+            block = loaded.tile([P, PACK, W], F32, name="block")
+            nc.sync.dma_start(out=block[:], in_=src)
+            return block
 
         load_x(0, 0)
-        for h in range(2):
-            weight[h] = keep.tile([P, W], F32, name="wgt_%d" % h)
+        weight = []
+        for h in range(PASSES):
+            weight.append(keep.tile([P, W], F32, name="wgt_%d" % h))
             nc.sync.dma_start(out=weight[h][:], in_=wgt[:, h * W : (h + 1) * W])
-        w1_rows = w1.rearrange("(a p j) r -> a p j r", a=2, j=PACK)
-        w1_raw = {}
         for a, i in ((0, 1), (0, 2), (0, 3), (1, 0), (1, 1)):
             load_x(a, i)
-        w1_raw[0, 0] = load_rows(w1_rows[0][:, :, 0:W])
-        bias = keep.tile([P, 2, PACK], F32, name="bias")
-        nc.sync.dma_start(out=bias[:], in_=b1.rearrange("(b p t) -> p b t", b=2, t=PACK))
+        w1_rows = w1.rearrange("(a p i) r -> a p i r", a=PASSES, i=PACK)
+        w1_block = {(0, 0): load_block(w1_rows[0][:, :, 0:W])}
+        bias = keep.tile([P, PASSES, PACK], F32, name="bias")
+        nc.sync.dma_start(out=bias[:], in_=b1.rearrange("(b p t) -> p b t", b=PASSES, t=PACK))
         load_x(1, 2)
+        w10_left = keep.tile([P, PACK, W // 2], F32, name="w10_left_then_x11", align_bytes=64)
+        nc.sync.dma_start(out=w10_left[:], in_=w1_rows[1][:, :, 0 : W // 2])
         load_x(1, 3)
-        w10_half = []
-        for u in range(2):
-            half = keep.tile([P, PACK, W // 2], F32, name="w10_half_%d" % u, align_bytes=64)
-            nc.sync.dma_start(out=half[:], in_=w1_rows[1][:, :, u * (W // 2) : (u + 1) * (W // 2)])
-            w10_half.append(half)
-        for a in range(2):
-            w1_raw[a, 1] = load_rows(w1_rows[a][:, :, W : 2 * W])
+        w10_right = keep.tile([P, PACK, W // 2], F32, name="w10_right", align_bytes=64)
+        nc.sync.dma_start(out=w10_right[:], in_=w1_rows[1][:, :, W // 2 : W])
+        for a in range(PASSES):
+            w1_block[a, 1] = load_block(w1_rows[a][:, :, W : 2 * W])
         for q in range(4):
             nc.sync.dma_start(
-                out=wa_plane[32 * q : 32 * q + 4].bitcast(I32),
-                in_=wa_scales[:, 4 * q : 4 * q + 4, :].rearrange("a r c -> r a c").bitcast(I32),
+                out=wa_scale_rows[32 * q : 32 * q + 4].bitcast(I32),
+                in_=wa_scales[:, 4 * q : 4 * q + 4, :].rearrange("b r n -> r b n").bitcast(I32),
             )
-        wb_rows = wb.rearrange("(b p j) n -> b p j n", b=2, j=PACK)
-        wb_raw = {}
-        wb_raw[0] = load_rows(wb_rows[0])
-        wa_codes = keep.tile([P, 2, 2 * N], U8, name="wa_codes", align_bytes=64)
-        nc.sync.dma_start(out=wa_codes[:].bitcast(I32), in_=wa_words.rearrange("a p c -> p a c").bitcast(I32))
-        wb_raw[1] = load_rows(wb_rows[1])
+        wb_rows = wb.rearrange("(b p t) n -> b p t n", b=PASSES, t=PACK)
+        wb_block = [load_block(wb_rows[0])]
+        wa_codes = keep.tile([P, PASSES, 2 * N], U8, name="wa_codes", align_bytes=64)
+        nc.sync.dma_start(out=wa_codes[:].bitcast(I32), in_=wa_words.rearrange("b p c -> p b c").bitcast(I32))
+        wb_block.append(load_block(wb_rows[1]))
         drive_rows = drive.rearrange("(g p) j -> p g j", p=P)
         out_rows = out.rearrange("(g p) j -> p g j", p=P)
-        result = {}
-        for h in range(2):
-            result[h] = load_rows(drive_rows[:, :, h * W : (h + 1) * W])
+        result = [load_block(drive_rows[:, :, h * W : (h + 1) * W]) for h in range(PASSES)]
 
-        def woven_tile(ring):
-            if ring is None:
-                return woven.tile([P, W, PACK], BF16, name="woven_rows", align_bytes=64)
-            return keep.tile([P, W, PACK], BF16, name="ring_%d" % ring, align_bytes=64)
+        def woven_tile(place=None):
+            if place is None:
+                return woven.tile([P, W, PACK], BF16, name="woven_tile", align_bytes=64)
+            return keep.tile([P, W, PACK], BF16, name=place, align_bytes=64)
 
-        def weave_views(dst, src, cols=slice(0, W)):
-            return (dst[:, cols, :].rearrange("p (c i) t -> p c t i", i=4), src[:, :, cols].rearrange("p t (c i) -> p c t i", i=4))
+        def weave_views(dst, src):
+            return dst[:].rearrange("p (c u) t -> p c t u", u=RUN), src[:].rearrange("p t (c u) -> p c t u", u=RUN)
 
-        def copy_on(engine, o, i):
-            if engine == "v":
-                nc.vector.tensor_copy(out=o, in_=i)
-            else:
-                nc.scalar.copy(out=o, in_=i)
-
-        def weave(engine, src, ring=None):
-            dst = woven_tile(ring)
-            copy_on(engine, *weave_views(dst, src))
+        def weave(copy, src, place=None):
+            dst = woven_tile(place)
+            woven_view, plane_view = weave_views(dst, src)
+            copy(out=woven_view, in_=plane_view)
             return dst
 
-        def weave_w1(engine, src, ring=None):
-            dst = woven_tile(ring)
-            copy_on(engine, dst[:].rearrange("p (t m) j -> p m j t", t=PACK), src[:].rearrange("p j (m t) -> p m j t", t=PACK))
+        def w1_woven_view(dst):
+            return dst[:].rearrange("p (t m) i -> p m i t", t=PACK)
+
+        def w1_plane_view(src):
+            return src[:].rearrange("p i (m t) -> p m i t", t=PACK)
+
+        def weave_w1(copy, src, place=None):
+            dst = woven_tile(place)
+            copy(out=w1_woven_view(dst), in_=w1_plane_view(src))
             return dst
 
-        def quantise(src, name, codes_name=None):
-            codes = keep.tile([P, W], U32, name=codes_name or name + "_codes", align_bytes=64)
+        def quantise(src, name):
+            codes = keep.tile([P, W], U32, name=name + "_codes", align_bytes=64)
             scales = keep.tile([P, W], U8, name=name + "_scales", align_bytes=64)
-            nc.vector.quantize_mx(out=codes[:].bitcast(FP8X4), scales=scales[:], in_=src[:].rearrange("p w j -> p (w j)"))
+            nc.vector.quantize_mx(out=codes[:].bitcast(FP8X4), scales=scales[:], in_=src[:].rearrange("p c t -> p (c t)"))
             return codes, scales
 
         picked = {}
 
         def gather(a, i, h):
             if i == 0:
-                picked[a, h] = planes4.tile([P, PACK, W], F32, name="planes")
-            nc.vector.tensor_tensor(
-                picked[a, h][:, i, :],
-                x_plane[a, i][:].indirect(offsets[:, h * (W // 16) : (h + 1) * (W // 16)]),
-                weight[h][:],
-                MULT,
-            )
+                picked[a, h] = planes.tile([P, PACK, W], F32, name="four_planes")
+            window = x_plane[a, i][:].indirect(offsets[:, h * LIST_COLUMNS : (h + 1) * LIST_COLUMNS])
+            nc.vector.tensor_tensor(picked[a, h][:, i, :], window, weight[h][:], MULT)
 
-        xq, w1q, wbq, zq, sq = {}, {}, {}, {}, {}
-        xw = {}
-        for i in range(PACK):
-            for h in range(2):
-                gather(0, i, h)
-        for h in range(2):
-            xw[0, h] = weave("s", picked[0, h])
-        w00 = weave_w1("s", w1_raw[0, 0])
-        gather(1, 0, 0)
-        gather(1, 0, 1)
-        xq[0, 0] = quantise(xw[0, 0], "xq00")
-        gather(1, 1, 0)
-        gather(1, 1, 1)
-        xq[0, 1] = quantise(xw[0, 1], "xq01")
-        gather(1, 2, 0)
-        gather(1, 2, 1)
-        w1q[0, 0] = quantise(w00, "w1q00")
-        gather(1, 3, 0)
-        xw[1, 0] = woven_tile(0)
-        copy_on("s", *weave_views(xw[1, 0], picked[1, 0], slice(0, W // 2)))
-        copy_on("v", *weave_views(xw[1, 0], picked[1, 0], slice(W // 2, W)))
-        gather(1, 3, 1)
-        xq[1, 0] = quantise(xw[1, 0], "xq10")
-        w10 = woven_tile(1)
-        for u, engine in enumerate("sv"):
-            copy_on(
-                engine,
-                w10[:].rearrange("p (t m) j -> p m j t", t=PACK)[:, u * (P // 2) : (u + 1) * (P // 2)],
-                w10_half[u][:].rearrange("p j (m t) -> p m j t", t=PACK),
-            )
-        w1q[1, 0] = quantise(w10, "w1q10")
-        xw[1, 1] = keep.tile([P, W, PACK], BF16, name="w10_half_0", align_bytes=64)
-        copy_on("s", *weave_views(xw[1, 1], picked[1, 1]))
+        def gather_both_halves(a, i):
+            for h in range(PASSES):
+                gather(a, i, h)
 
         def four_banks(side):
             return [psum.tile([P, W], F32, name="bank_%d" % (4 * side + t)) for t in range(4)]
 
-        def lift(b, h, side, pass_major):
+        xq, w1q, wbq, zq, sq = {}, {}, {}, {}, {}
+        bank_major = [(t, a) for t in range(PACK) for a in range(PASSES)]
+        pass_major = [(t, a) for a in range(PASSES) for t in range(PACK)]
+
+        def lift(b, h, side, order, place=None):
             banks = four_banks(side)
-            order = [(t, a) for t in range(PACK) for a in range(2)]
-            if pass_major:
-                order = [(t, a) for a in range(2) for t in range(PACK)]
-            z32 = planes4.tile([P, PACK, W], F32, name="planes")
+            if place is None:
+                z = planes.tile([P, PACK, W], F32, name="four_planes")
+            else:
+                z = keep.tile([P, PACK, W], F32, name=place, align_bytes=64)
             for t, a in order:
-                cols = slice(t * P, (t + 1) * P)
+                columns = slice(t * P, (t + 1) * P)
                 nc.tensor.matmul_mx(
                     out=banks[t][:],
-                    lhsT=w1q[a, b][0][:, cols].bitcast(FP8X4),
-                    lhsT_scale=w1q[a, b][1][:, cols],
+                    lhsT=w1q[a, b][0][:, columns].bitcast(FP8X4),
+                    lhsT_scale=w1q[a, b][1][:, columns],
                     rhs=xq[a, h][0][:].bitcast(FP8X4),
                     rhs_scale=xq[a, h][1][:],
                     start=(a == 0),
-                    stop=(a == 1),
+                    stop=(a == PASSES - 1),
                 )
-                if a == 1:
-                    nc.scalar.activation(out=z32[:, t, :], in_=banks[t][:], func=IDENTITY, bias=bias[:, b, t : t + 1])
-            return z32
+                if a == PASSES - 1:
+                    nc.scalar.activation(out=z[:, t, :], in_=banks[t][:], func=IDENTITY, bias=bias[:, b, t : t + 1])
+            return z
 
-        def square(z32):
-            dst = woven_tile(None)
-            o, i = weave_views(dst, z32)
-            nc.scalar.activation(out=o, in_=i, func=SQUARE)
+        def weave_square(z, place=None):
+            dst = woven_tile(place)
+            woven_view, plane_view = weave_views(dst, z)
+            nc.scalar.activation(out=woven_view, in_=plane_view, func=SQUARE)
             return dst
 
-        ybanks = {}
-
-        def predict(b, h, kind):
-            if h not in ybanks:
-                ybanks[h] = four_banks(1 - h)
-            for g in range(4):
-                cols = slice(g * P, (g + 1) * P)
-                if kind == "z":
-                    lhs = wa_codes[:, b, 2 * g * P : 2 * (g + 1) * P].bitcast(FP4X4)
-                    lhs_scale = wa_plane[:, b, cols]
-                    rhs = zq[b, h]
-                else:
-                    lhs = wbq[b][0][:, cols].bitcast(FP8X4)
-                    lhs_scale = wbq[b][1][:, cols]
-                    rhs = sq[b, h]
+        def linear_passes(y, b, h):
+            for g in range(GROUPS):
                 nc.tensor.matmul_mx(
-                    out=ybanks[h][g][:],
-                    lhsT=lhs,
-                    lhsT_scale=lhs_scale,
-                    rhs=rhs[0][:].bitcast(FP8X4),
-                    rhs_scale=rhs[1][:],
-                    start=(b == 0 and kind == "z"),
-                    stop=(b == 1 and kind == "s"),
+                    out=y[g][:],
+                    lhsT=wa_codes[:, b, 2 * g * P : 2 * (g + 1) * P].bitcast(FP4X4),
+                    lhsT_scale=wa_scale_rows[:, b, g * P : (g + 1) * P],
+                    rhs=zq[b, h][0][:].bitcast(FP8X4),
+                    rhs_scale=zq[b, h][1][:],
+                    start=(b == 0),
+                    stop=False,
                 )
 
-        def finish(h, g):
-            nc.vector.tensor_tensor(result[h][:, g, :], ybanks[h][g][:], result[h][:, g, :], ADD)
-            nc.sync.dma_start(out=out_rows[:, g, h * W : (h + 1) * W], in_=result[h][:, g, :])
+        def quadratic_passes(y, b, h, last):
+            for g in range(GROUPS):
+                columns = slice(g * P, (g + 1) * P)
+                nc.tensor.matmul_mx(
+                    out=y[g][:],
+                    lhsT=wbq[b][0][:, columns].bitcast(FP8X4),
+                    lhsT_scale=wbq[b][1][:, columns],
+                    rhs=sq[b, h][0][:].bitcast(FP8X4),
+                    rhs_scale=sq[b, h][1][:],
+                    start=False,
+                    stop=last,
+                )
 
-        z00 = lift(0, 0, 0, True)
-        s00 = square(z00)
-        w01 = weave_w1("v", w1_raw[0, 1], 0)
-        xq[1, 1] = quantise(xw[1, 1], "xq11")
+        on_vector, on_scalar = nc.vector.tensor_copy, nc.scalar.copy
+
+        for i in range(PACK):
+            gather_both_halves(0, i)
+        x00 = weave(on_scalar, picked[0, 0])
+        x01 = weave(on_scalar, picked[0, 1])
+        w00 = weave_w1(on_scalar, w1_block[0, 0])
+        gather_both_halves(1, 0)
+        xq[0, 0] = quantise(x00, "xq00")
+        gather_both_halves(1, 1)
+        xq[0, 1] = quantise(x01, "xq01")
+        gather_both_halves(1, 2)
+        w1q[0, 0] = quantise(w00, "w1q00")
+        gather(1, 3, 0)
+        x10 = weave(on_scalar, picked[1, 0], "ring_0")
+        gather(1, 3, 1)
+        xq[1, 0] = quantise(x10, "xq10")
+        w10 = woven_tile("ring_1")
+        on_scalar(out=w1_woven_view(w10)[:, 0 : P // 2], in_=w1_plane_view(w10_left))
+        on_vector(out=w1_woven_view(w10)[:, P // 2 : P], in_=w1_plane_view(w10_right))
+        w1q[1, 0] = quantise(w10, "w1q10")
+        x11 = weave(on_scalar, picked[1, 1], "w10_left_then_x11")
+
+        z00 = lift(0, 0, 0, pass_major)
+        s00 = weave_square(z00)
+        w01 = weave_w1(on_vector, w1_block[0, 1], "ring_0")
+        xq[1, 1] = quantise(x11, "xq11")
         w1q[0, 1] = quantise(w01, "w1q01")
-        w11 = weave_w1("v", w1_raw[1, 1], 1)
-        zw = weave("v", z00, 0)
+        w11 = weave_w1(on_vector, w1_block[1, 1], "ring_1")
+        z00_woven = weave(on_vector, z00, "ring_0")
         w1q[1, 1] = quantise(w11, "w1q11")
-        zq[0, 0] = quantise(zw, "zq00")
+        zq[0, 0] = quantise(z00_woven, "zq00")
 
-        z01 = lift(0, 1, 1, False)
-        s01 = square(z01)
-        wb0 = weave("v", wb_raw[0], 1)
+        z01 = lift(0, 1, 1, bank_major)
+        wb0 = weave(on_vector, wb_block[0], "ring_1")
         sq[0, 0] = quantise(s00, "sq00")
-        zw = weave("v", z01, 0)
+        z01_woven = weave(on_vector, z01, "ring_0")
         wbq[0] = quantise(wb0, "wbq0")
-        zq[0, 1] = quantise(zw, "zq01")
 
-        z10 = lift(1, 0, 0, False)
-        s10 = square(z10)
-        predict(0, 0, "z")
-        predict(0, 0, "s")
-        wb1 = weave("v", wb_raw[1], 1)
-        sq[0, 1] = quantise(s01, "sq01")
-        zw = weave("v", z10, 0)
+        z10 = lift(1, 0, 0, bank_major, "z10_then_s01")
+        s10 = weave_square(z10)
+        y0 = four_banks(1)
+        linear_passes(y0, 0, 0)
+        quadratic_passes(y0, 0, 0, False)
+        wb1 = weave(on_vector, wb_block[1], "ring_1")
+        zq[0, 1] = quantise(z01_woven, "zq01")
+        z10_woven = weave(on_vector, z10, "ring_0")
         wbq[1] = quantise(wb1, "wbq1")
-        zq[1, 0] = quantise(zw, "zq10")
-
-        z11 = lift(1, 1, 0, False)
-        s11 = square(z11)
+        zq[1, 0] = quantise(z10_woven, "zq10")
         sq[1, 0] = quantise(s10, "sq10")
-        predict(1, 0, "z")
-        predict(1, 0, "s")
-        finish(0, 0)
-        finish(0, 1)
-        zw = weave("v", z11, 1)
-        finish(0, 2)
-        zq[1, 1] = quantise(zw, "zq11")
-        finish(0, 3)
-        predict(0, 1, "z")
-        predict(0, 1, "s")
-        predict(1, 1, "z")
+        linear_passes(y0, 1, 0)
+        quadratic_passes(y0, 1, 0, True)
+
+        z11 = lift(1, 1, 0, bank_major)
+        s01 = weave_square(z01, "z10_then_s01")
+        s11 = weave_square(z11)
+        z11_woven = weave(on_vector, z11, "ring_1")
+        y1 = four_banks(0)
+        linear_passes(y1, 0, 1)
+        zq[1, 1] = quantise(z11_woven, "zq11")
+        linear_passes(y1, 1, 1)
+        sq[0, 1] = quantise(s01, "sq01")
+        quadratic_passes(y1, 0, 1, False)
         sq[1, 1] = quantise(s11, "sq11")
-        predict(1, 1, "s")
-        for g in range(4):
-            finish(1, g)
+        quadratic_passes(y1, 1, 1, True)
+
+        for h, y in enumerate((y0, y1)):
+            for g in range(GROUPS):
+                nc.vector.tensor_tensor(result[h][:, g, :], y[g][:], result[h][:, g, :], ADD)
+                nc.sync.dma_start(out=out_rows[:, g, h * W : (h + 1) * W], in_=result[h][:, g, :])

@@ -1,6 +1,7 @@
 from contextlib import ExitStack
 
 import concourse.mybir as mybir
+from concourse.masks import make_identity
 
 K, T, S, H, N = 1024, 2048, 1024, 1024, 512
 FLOPS = 2 * K * H * S + 2 * 2 * H * N * S
@@ -25,19 +26,33 @@ W = 512
 GROUPS = N // P
 RUN = 4
 LIST_COLUMNS = W // 16
+HEADS = 8
+SHARE = P // HEADS
 
 
 def tile_list_koopman_delay_lift_kernel(tc, xT, wgt, offs, w1, b1, wa_words, wa_scales, wb, drive, out):
     nc = tc.nc
     with ExitStack() as ctx:
         keep = ctx.enter_context(tc.tile_pool(name="keep", bufs=1))
-        loaded = ctx.enter_context(tc.tile_pool(name="loaded", bufs=5))
-        planes = ctx.enter_context(tc.tile_pool(name="planes", bufs=4))
-        woven = ctx.enter_context(tc.tile_pool(name="woven", bufs=4))
         psum = ctx.enter_context(tc.psum_pool(name="psum", bufs=1))
+        on_vector, on_scalar = nc.vector.tensor_copy, nc.scalar.copy
+
+        def bank(n):
+            return psum.tile([P, W], F32, name="bank_%d" % n)
+
+        def big(place):
+            return keep.tile([P, PACK, W], F32, name=place, align_bytes=64)
 
         offsets = keep.tile([P, S // 16], U16, name="offsets")
         nc.sync.dma_start(offsets[:], offs)
+
+        wgt_rows = keep.tile([P, P], F32, name="wgt_rows")
+        nc.sync.dma_start(
+            out=wgt_rows[:],
+            in_=wgt.rearrange("(g s) j -> g (s j)", s=SHARE)[:, 0 : SHARE * P].rearrange("g (u j) -> g u j", j=P),
+        )
+        identity = keep.tile([P, P], F32, name="identity")
+        make_identity(nc, identity[:])
 
         wa_scale_rows = keep.tile([P, PASSES, N], U8, name="wa_scale_rows", align_bytes=64)
         nc.vector.memset(wa_scale_rows[:].bitcast(I32), 0)
@@ -46,75 +61,97 @@ def tile_list_koopman_delay_lift_kernel(tc, xT, wgt, offs, w1, b1, wa_words, wa_
         x_plane = {}
 
         def load_x(a, i):
-            x_plane[a, i] = keep.tile([P, T], F32, name="x_%d_%d" % (a, i))
+            x_plane[a, i] = keep.tile([P, T], F32, name="x_%d_%d" % (a, i), align_bytes=64)
             nc.sync.dma_start(out=x_plane[a, i][:], in_=x_rows[a, i])
 
-        def load_block(src):
-            block = loaded.tile([P, PACK, W], F32, name="block")
+        def load_block(src, place):
+            block = big(place)
             nc.sync.dma_start(out=block[:], in_=src)
             return block
 
+        w1_rows = w1.rearrange("(a p i) r -> a p i r", a=PASSES, i=PACK)
+        w1_block = {}
+
+        def load_w1(a, b):
+            w1_block[a, b] = load_block(w1_rows[a][:, :, b * W : (b + 1) * W], "w1_%d_%d" % (a, b))
+
         load_x(0, 0)
-        weight = []
-        for h in range(PASSES):
-            weight.append(keep.tile([P, W], F32, name="wgt_%d" % h))
-            nc.sync.dma_start(out=weight[h][:], in_=wgt[:, h * W : (h + 1) * W])
         for a, i in ((0, 1), (0, 2), (0, 3), (1, 0), (1, 1)):
             load_x(a, i)
-        w1_rows = w1.rearrange("(a p i) r -> a p i r", a=PASSES, i=PACK)
-        w1_block = {(0, 0): load_block(w1_rows[0][:, :, 0:W])}
+        load_w1(0, 0)
+        load_x(1, 2)
+        w10_half = []
+        for u in range(2):
+            w10_half.append(keep.tile([P, PACK, W // 2], F32, name="w1_1_0_%d" % u, align_bytes=64))
+            nc.sync.dma_start(out=w10_half[u][:], in_=w1_rows[1][:, :, u * W // 2 : (u + 1) * W // 2])
+            if u == 0:
+                load_x(1, 3)
         bias = keep.tile([P, PASSES, PACK], F32, name="bias")
         nc.sync.dma_start(out=bias[:], in_=b1.rearrange("(b p t) -> p b t", b=PASSES, t=PACK))
-        load_x(1, 2)
-        w10_left = keep.tile([P, PACK, W // 2], F32, name="w10_left_then_x11", align_bytes=64)
-        nc.sync.dma_start(out=w10_left[:], in_=w1_rows[1][:, :, 0 : W // 2])
-        load_x(1, 3)
-        w10_right = keep.tile([P, PACK, W // 2], F32, name="w10_right", align_bytes=64)
-        nc.sync.dma_start(out=w10_right[:], in_=w1_rows[1][:, :, W // 2 : W])
-        for a in range(PASSES):
-            w1_block[a, 1] = load_block(w1_rows[a][:, :, W : 2 * W])
+        load_w1(0, 1)
+        load_w1(1, 1)
+        wb_rows = wb.rearrange("(b p t) n -> b p t n", b=PASSES, t=PACK)
+        wb_block = [load_block(wb_rows[0], "wb_0")]
+        wb_block.append(load_block(wb_rows[1], "wb_1"))
+        wa_codes = keep.tile([P, PASSES, 2 * N], U8, name="wa_codes", align_bytes=64)
+        nc.sync.dma_start(out=wa_codes[:].bitcast(I32), in_=wa_words.rearrange("b p c -> p b c").bitcast(I32))
         for q in range(4):
             nc.sync.dma_start(
                 out=wa_scale_rows[32 * q : 32 * q + 4].bitcast(I32),
                 in_=wa_scales[:, 4 * q : 4 * q + 4, :].rearrange("b r n -> r b n").bitcast(I32),
             )
-        wb_rows = wb.rearrange("(b p t) n -> b p t n", b=PASSES, t=PACK)
-        wb_block = [load_block(wb_rows[0])]
-        wa_codes = keep.tile([P, PASSES, 2 * N], U8, name="wa_codes", align_bytes=64)
-        nc.sync.dma_start(out=wa_codes[:].bitcast(I32), in_=wa_words.rearrange("b p c -> p b c").bitcast(I32))
-        wb_block.append(load_block(wb_rows[1]))
-        drive_rows = drive.rearrange("(g p) j -> p g j", p=P)
-        out_rows = out.rearrange("(g p) j -> p g j", p=P)
-        result = [load_block(drive_rows[:, :, h * W : (h + 1) * W]) for h in range(PASSES)]
 
-        def woven_tile(place=None):
-            if place is None:
-                return woven.tile([P, W, PACK], BF16, name="woven_tile", align_bytes=64)
-            return keep.tile([P, W, PACK], BF16, name=place, align_bytes=64)
+        weight = [keep.tile([P, W], F32, name="weight_%d" % h) for h in range(PASSES)]
+
+        def turn(n):
+            turned = bank(n)
+            nc.tensor.transpose(turned[:, 0:P], wgt_rows[:], identity[:])
+            return turned[:, 0:P].rearrange("j (g u) -> j u g", u=SHARE)
+
+        def spread_weight(copy, by_head, first, count, n):
+            spread = keep.tile([P, count, HEADS, SHARE], F32, name="spread_%d" % first)
+            copy(out=spread[:], in_=by_head[:, first : first + count, :].unsqueeze(3).to_broadcast([P, count, HEADS, SHARE]))
+            back = bank(n)
+            for c in range(count):
+                nc.tensor.transpose(back[:, c * P : (c + 1) * P], spread[:, c].rearrange("j g s -> j (g s)"), identity[:])
+            lo = first % PACK * P
+            copy(out=weight[first // PACK][:, lo : lo + count * P], in_=back[:, 0 : count * P])
+
+        for_vector, for_scalar = turn(0), turn(1)
+        spread_weight(on_vector, for_vector, 0, 2, 2)
+        spread_weight(on_scalar, for_scalar, 2, 2, 3)
+        spread_weight(on_scalar, for_scalar, 4, 4, 4)
+
+        def woven_tile(place, width=W):
+            return keep.tile([P, width, PACK], BF16, name=place, align_bytes=64)
 
         def weave_views(dst, src):
-            return dst[:].rearrange("p (c u) t -> p c t u", u=RUN), src[:].rearrange("p t (c u) -> p c t u", u=RUN)
+            return dst.rearrange("p (c u) t -> p c t u", u=RUN), src.rearrange("p t (c u) -> p c t u", u=RUN)
 
-        def weave(copy, src, place=None):
+        def weave(copy, src, place):
             dst = woven_tile(place)
-            woven_view, plane_view = weave_views(dst, src)
+            woven_view, plane_view = weave_views(dst[:], src)
             copy(out=woven_view, in_=plane_view)
             return dst
+
+        def weave_pair(dst, src, first):
+            woven_view, plane_view = weave_views(dst[:, :, first : first + 2], src[:, first : first + 2, :])
+            on_scalar(out=woven_view, in_=plane_view)
 
         def w1_woven_view(dst):
             return dst[:].rearrange("p (t m) i -> p m i t", t=PACK)
 
         def w1_plane_view(src):
-            return src[:].rearrange("p i (m t) -> p m i t", t=PACK)
+            return src.rearrange("p i (m t) -> p m i t", t=PACK)
 
-        def weave_w1(copy, src, place=None):
+        def weave_w1(copy, src, place):
             dst = woven_tile(place)
             copy(out=w1_woven_view(dst), in_=w1_plane_view(src))
             return dst
 
-        def quantise(src, name):
-            codes = keep.tile([P, W], U32, name=name + "_codes", align_bytes=64)
-            scales = keep.tile([P, W], U8, name=name + "_scales", align_bytes=64)
+        def quantise(src, name, width=W, place=None):
+            codes = keep.tile([P, width], U32, name=place or name + "_codes", align_bytes=64)
+            scales = keep.tile([P, width], U8, name=name + "_scales", align_bytes=64)
             nc.vector.quantize_mx(out=codes[:].bitcast(FP8X4), scales=scales[:], in_=src[:].rearrange("p c t -> p (c t)"))
             return codes, scales
 
@@ -122,7 +159,7 @@ def tile_list_koopman_delay_lift_kernel(tc, xT, wgt, offs, w1, b1, wa_words, wa_
 
         def gather(a, i, h):
             if i == 0:
-                picked[a, h] = planes.tile([P, PACK, W], F32, name="four_planes")
+                picked[a, h] = big("picked_%d_%d" % (a, h))
             window = x_plane[a, i][:].indirect(offsets[:, h * LIST_COLUMNS : (h + 1) * LIST_COLUMNS])
             nc.vector.tensor_tensor(picked[a, h][:, i, :], window, weight[h][:], MULT)
 
@@ -130,132 +167,177 @@ def tile_list_koopman_delay_lift_kernel(tc, xT, wgt, offs, w1, b1, wa_words, wa_
             for h in range(PASSES):
                 gather(a, i, h)
 
-        def four_banks(side):
-            return [psum.tile([P, W], F32, name="bank_%d" % (4 * side + t)) for t in range(4)]
-
         xq, w1q, wbq, zq, sq = {}, {}, {}, {}, {}
-        bank_major = [(t, a) for t in range(PACK) for a in range(PASSES)]
-        pass_major = [(t, a) for a in range(PASSES) for t in range(PACK)]
 
-        def lift(b, h, side, order, place=None):
-            banks = four_banks(side)
-            if place is None:
-                z = planes.tile([P, PACK, W], F32, name="four_planes")
-            else:
-                z = keep.tile([P, PACK, W], F32, name=place, align_bytes=64)
-            for t, a in order:
-                columns = slice(t * P, (t + 1) * P)
-                nc.tensor.matmul_mx(
-                    out=banks[t][:],
-                    lhsT=w1q[a, b][0][:, columns].bitcast(FP8X4),
-                    lhsT_scale=w1q[a, b][1][:, columns],
-                    rhs=xq[a, h][0][:].bitcast(FP8X4),
-                    rhs_scale=xq[a, h][1][:],
-                    start=(a == 0),
-                    stop=(a == PASSES - 1),
-                )
-                if a == PASSES - 1:
-                    nc.scalar.activation(out=z[:, t, :], in_=banks[t][:], func=IDENTITY, bias=bias[:, b, t : t + 1])
+        def lift_pass(banks, a, b, h, t):
+            columns = slice(t * P, (t + 1) * P)
+            nc.tensor.matmul_mx(
+                out=banks[t][:],
+                lhsT=w1q[a, b][0][:, columns].bitcast(FP8X4),
+                lhsT_scale=w1q[a, b][1][:, columns],
+                rhs=xq[a, h][0][:].bitcast(FP8X4),
+                rhs_scale=xq[a, h][1][:],
+                start=(a == 0),
+                stop=(a == PASSES - 1),
+            )
+
+        def open_unit(b, h, side):
+            banks = [bank(4 * side + t) for t in range(PACK)]
+            for t in range(PACK):
+                lift_pass(banks, 0, b, h, t)
+            return banks
+
+        def close_unit(banks, b, h, place):
+            z = big(place)
+            for t in range(PACK):
+                lift_pass(banks, 1, b, h, t)
+                nc.scalar.activation(out=z[:, t, :], in_=banks[t][:], func=IDENTITY, bias=bias[:, b, t : t + 1])
             return z
 
-        def weave_square(z, place=None):
-            dst = woven_tile(place)
-            woven_view, plane_view = weave_views(dst, z)
+        def weave_square(z, place, width=W):
+            dst = woven_tile(place, width)
+            woven_view, plane_view = weave_views(dst[:], z)
             nc.scalar.activation(out=woven_view, in_=plane_view, func=SQUARE)
             return dst
 
-        def linear_passes(y, b, h):
-            for g in range(GROUPS):
-                nc.tensor.matmul_mx(
-                    out=y[g][:],
-                    lhsT=wa_codes[:, b, 2 * g * P : 2 * (g + 1) * P].bitcast(FP4X4),
-                    lhsT_scale=wa_scale_rows[:, b, g * P : (g + 1) * P],
-                    rhs=zq[b, h][0][:].bitcast(FP8X4),
-                    rhs_scale=zq[b, h][1][:],
-                    start=(b == 0),
-                    stop=False,
-                )
+        def linear_pass(y, b, g, z, start):
+            nc.tensor.matmul_mx(
+                out=y,
+                lhsT=wa_codes[:, b, 2 * g * P : 2 * (g + 1) * P].bitcast(FP4X4),
+                lhsT_scale=wa_scale_rows[:, b, g * P : (g + 1) * P],
+                rhs=z[0].bitcast(FP8X4),
+                rhs_scale=z[1],
+                start=start,
+                stop=False,
+            )
 
-        def quadratic_passes(y, b, h, last):
-            for g in range(GROUPS):
-                columns = slice(g * P, (g + 1) * P)
-                nc.tensor.matmul_mx(
-                    out=y[g][:],
-                    lhsT=wbq[b][0][:, columns].bitcast(FP8X4),
-                    lhsT_scale=wbq[b][1][:, columns],
-                    rhs=sq[b, h][0][:].bitcast(FP8X4),
-                    rhs_scale=sq[b, h][1][:],
-                    start=False,
-                    stop=last,
-                )
+        def quadratic_pass(y, b, g, s, stop):
+            columns = slice(g * P, (g + 1) * P)
+            nc.tensor.matmul_mx(
+                out=y,
+                lhsT=wbq[b][0][:, columns].bitcast(FP8X4),
+                lhsT_scale=wbq[b][1][:, columns],
+                rhs=s[0].bitcast(FP8X4),
+                rhs_scale=s[1],
+                start=False,
+                stop=stop,
+            )
 
-        on_vector, on_scalar = nc.vector.tensor_copy, nc.scalar.copy
+        def part(q, lo, hi):
+            return q[0][:, lo:hi], q[1][:, lo:hi]
 
         for i in range(PACK):
             gather_both_halves(0, i)
-        x00 = weave(on_scalar, picked[0, 0])
-        x01 = weave(on_scalar, picked[0, 1])
-        w00 = weave_w1(on_scalar, w1_block[0, 0])
+        x0 = woven_tile("x0_woven", 2 * W)
+        for h in range(PASSES):
+            woven_view, plane_view = weave_views(x0[:, h * W : (h + 1) * W, :], picked[0, h][:])
+            on_scalar(out=woven_view, in_=plane_view)
         gather_both_halves(1, 0)
-        xq[0, 0] = quantise(x00, "xq00")
         gather_both_halves(1, 1)
-        xq[0, 1] = quantise(x01, "xq01")
+        both = quantise(x0, "xq0", 2 * W, place="x_1_1")
+        for h in range(PASSES):
+            xq[0, h] = part(both, h * W, (h + 1) * W)
+        w00 = weave_w1(on_scalar, w1_block[0, 0][:], "s_ring_2")
+        x1 = woven_tile("w1_0_0", 2 * W)
+        x10, x11 = x1[:, 0:W, :], x1[:, W : 2 * W, :]
+        weave_pair(x10, picked[1, 0], 0)
+        weave_pair(x11, picked[1, 1], 0)
+        w10 = woven_tile("v_ring_0")
+        on_scalar(out=w1_woven_view(w10)[:, 0 : P // 2], in_=w1_plane_view(w10_half[0][:]))
         gather_both_halves(1, 2)
-        w1q[0, 0] = quantise(w00, "w1q00")
+        w1q[0, 0] = quantise(w00, "w1q00", place="x_1_2")
+        unit00 = open_unit(0, 0, 0)
+        unit01 = open_unit(0, 1, 1)
         gather(1, 3, 0)
-        x10 = weave(on_scalar, picked[1, 0], "ring_0")
+        weave_pair(x10, picked[1, 0], 2)
         gather(1, 3, 1)
+        weave_pair(x11, picked[1, 1], 2)
+        on_vector(out=w1_woven_view(w10)[:, P // 2 : P], in_=w1_plane_view(w10_half[1][:]))
         xq[1, 0] = quantise(x10, "xq10")
-        w10 = woven_tile("ring_1")
-        on_scalar(out=w1_woven_view(w10)[:, 0 : P // 2], in_=w1_plane_view(w10_left))
-        on_vector(out=w1_woven_view(w10)[:, P // 2 : P], in_=w1_plane_view(w10_right))
-        w1q[1, 0] = quantise(w10, "w1q10")
-        x11 = weave(on_scalar, picked[1, 1], "w10_left_then_x11")
-
-        z00 = lift(0, 0, 0, pass_major)
-        s00 = weave_square(z00)
-        w01 = weave_w1(on_vector, w1_block[0, 1], "ring_0")
-        xq[1, 1] = quantise(x11, "xq11")
+        w1q[1, 0] = quantise(w10, "w1q10", place="x_0_2")
+        z00 = close_unit(unit00, 0, 0, "x_0_0")
+        w01 = weave_w1(on_vector, w1_block[0, 1][:], "v_ring_1")
+        xq[1, 1] = quantise(x11, "xq11", place="w1_0_1")
+        z01 = close_unit(unit01, 0, 1, "x_0_1")
         w1q[0, 1] = quantise(w01, "w1q01")
-        w11 = weave_w1(on_vector, w1_block[1, 1], "ring_1")
-        z00_woven = weave(on_vector, z00, "ring_0")
+        w11 = weave_w1(on_vector, w1_block[1, 1][:], "v_ring_0")
         w1q[1, 1] = quantise(w11, "w1q11")
-        zq[0, 0] = quantise(z00_woven, "zq00")
-
-        z01 = lift(0, 1, 1, bank_major)
-        wb0 = weave(on_vector, wb_block[0], "ring_1")
-        sq[0, 0] = quantise(s00, "sq00")
-        z01_woven = weave(on_vector, z01, "ring_0")
+        z00w = weave(on_vector, z00[:], "w1_1_1")
+        s00 = weave_square(z00[:], "x_0_2")
+        z10 = close_unit(open_unit(1, 0, 0), 1, 0, "picked_0_0")
+        wb0 = weave(on_vector, wb_block[0][:], "v_ring_1")
+        zq[0, 0] = quantise(z00w, "zq00")
         wbq[0] = quantise(wb0, "wbq0")
-
-        z10 = lift(1, 0, 0, bank_major, "z10_then_s01")
-        s10 = weave_square(z10)
-        y0 = four_banks(1)
-        linear_passes(y0, 0, 0)
-        quadratic_passes(y0, 0, 0, False)
-        wb1 = weave(on_vector, wb_block[1], "ring_1")
-        zq[0, 1] = quantise(z01_woven, "zq01")
-        z10_woven = weave(on_vector, z10, "ring_0")
+        sq[0, 0] = quantise(s00, "sq00")
+        wb1 = weave(on_vector, wb_block[1][:], "v_ring_0")
         wbq[1] = quantise(wb1, "wbq1")
-        zq[1, 0] = quantise(z10_woven, "zq10")
-        sq[1, 0] = quantise(s10, "sq10")
-        linear_passes(y0, 1, 0)
-        quadratic_passes(y0, 1, 0, True)
+        s10 = weave_square(z10[:], "s_ring_3")
+        z10w = weave(on_vector, z10[:], "wb_1")
+        zq[1, 0] = quantise(z10w, "zq10")
+        z01w = weave(on_vector, z01[:], "wb_1")
+        sq[1, 0] = quantise(s10, "sq10", place="picked_0_0")
+        zq[0, 1] = quantise(z01w, "zq01")
 
-        z11 = lift(1, 1, 0, bank_major)
-        s01 = weave_square(z01, "z10_then_s01")
-        s11 = weave_square(z11)
-        z11_woven = weave(on_vector, z11, "ring_1")
-        y1 = four_banks(0)
-        linear_passes(y1, 0, 1)
-        zq[1, 1] = quantise(z11_woven, "zq11")
-        linear_passes(y1, 1, 1)
-        sq[0, 1] = quantise(s01, "sq01")
-        quadratic_passes(y1, 0, 1, False)
-        sq[1, 1] = quantise(s11, "sq11")
-        quadratic_passes(y1, 1, 1, True)
+        drive_rows = drive.rearrange("(g p) j -> p g j", p=P)
+        out_rows = out.rearrange("(g p) j -> p g j", p=P)
+        result = [load_block(drive_rows[:, :, h * W : (h + 1) * W], ("x_1_0", "x_1_3")[h]) for h in range(PASSES)]
 
-        for h, y in enumerate((y0, y1)):
+        y0 = [bank(4 + g) for g in range(GROUPS)]
+        for g in range(GROUPS):
+            linear_pass(y0[g][:], 0, g, part(zq[0, 0], 0, W), True)
+        for g in range(GROUPS):
+            quadratic_pass(y0[g][:], 0, g, part(sq[0, 0], 0, W), False)
+        z11 = close_unit(open_unit(1, 1, 0), 1, 1, "x_0_3")
+        for g in range(GROUPS):
+            linear_pass(y0[g][:], 1, g, part(zq[1, 0], 0, W), False)
+        for g in range(GROUPS):
+            quadratic_pass(y0[g][:], 1, g, part(sq[1, 0], 0, W), True)
+
+        def finish_half0(g):
+            nc.vector.tensor_tensor(result[0][:, g, :], y0[g][:], result[0][:, g, :], ADD)
+            nc.sync.dma_start(out=out_rows[:, g, 0:W], in_=result[0][:, g, :])
+
+        Q = W // 2
+        y1 = [[bank(2 * u + v) for v in range(2)] for u in range(2)]
+
+        def y1_view(u, g):
+            return y1[u][g // 2][:, (g % 2) * Q : (g % 2 + 1) * Q]
+
+        def linear_quarter(b, u):
             for g in range(GROUPS):
-                nc.vector.tensor_tensor(result[h][:, g, :], y[g][:], result[h][:, g, :], ADD)
-                nc.sync.dma_start(out=out_rows[:, g, h * W : (h + 1) * W], in_=result[h][:, g, :])
+                linear_pass(y1_view(u, g), b, g, part(zq[b, 1], u * Q, (u + 1) * Q), b == 0 and g % 2 == 0)
+
+        def quadratic_quarter(b, u, woven):
+            codes = quantise(woven, "sq%d1_%d" % (b, u), Q)
+            for g in range(GROUPS):
+                quadratic_pass(y1_view(u, g), b, g, part(codes, 0, Q), b == 1 and g % 2 == 1)
+
+        def finish_quarter(u, v):
+            rows = keep.tile([P, 2, Q], F32, name=("wb_0", "picked_0_1", "picked_1_0", "picked_1_1")[2 * u + v], align_bytes=64)
+            nc.vector.tensor_tensor(
+                rows[:], y1[u][v][:].rearrange("p (g j) -> p g j", g=2), result[1][:, 2 * v : 2 * v + 2, u * Q : (u + 1) * Q], ADD
+            )
+            nc.sync.dma_start(out=out_rows[:, 2 * v : 2 * v + 2, W + u * Q : W + (u + 1) * Q], in_=rows[:])
+
+        squares = {}
+        for u in range(2):
+            for b, z in enumerate((z01, z11)):
+                squares[b, u] = weave_square(z[:, :, u * Q : (u + 1) * Q], (("w1q11_codes", "s_ring_2"), ("w1_0_1", "v_ring_1"))[u][b], Q)
+        finish_half0(0)
+        linear_quarter(0, 0)
+        linear_quarter(0, 1)
+        z11w = weave(on_vector, z11[:], "v_ring_0")
+        finish_half0(1)
+        zq[1, 1] = quantise(z11w, "zq11")
+        linear_quarter(1, 0)
+        quadratic_quarter(0, 0, squares[0, 0])
+        finish_half0(2)
+        quadratic_quarter(1, 0, squares[1, 0])
+        linear_quarter(1, 1)
+        finish_half0(3)
+        quadratic_quarter(0, 1, squares[0, 1])
+        finish_quarter(0, 0)
+        quadratic_quarter(1, 1, squares[1, 1])
+        finish_quarter(0, 1)
+        finish_quarter(1, 0)
+        finish_quarter(1, 1)

@@ -43,19 +43,25 @@ def tile_list_koopman_delay_lift_kernel(tc, xT, wgt, offs, w1, b1, wa_words, wa_
         def big(place):
             return keep.tile([P, PACK, W], F32, name=place, align_bytes=64)
 
-        offsets = keep.tile([P, S // 16], U16, name="offsets")
-        nc.sync.dma_start(offsets[:], offs)
-
         wgt_rows = keep.tile([P, P], F32, name="wgt_rows")
         nc.sync.dma_start(
             out=wgt_rows[:],
             in_=wgt.rearrange("(g s) j -> g (s j)", s=SHARE)[:, 0 : SHARE * P].rearrange("g (u j) -> g u j", j=P),
         )
+        offsets = keep.tile([P, S // 16], U16, name="offsets")
+        nc.sync.dma_start(offsets[:], offs)
+
         identity = keep.tile([P, P], F32, name="identity")
         make_identity(nc, identity[:])
 
         wa_scale_rows = keep.tile([P, PASSES, N], U8, name="wa_scale_rows", align_bytes=64)
-        nc.vector.memset(wa_scale_rows[:].bitcast(I32), 0)
+        nc.gpsimd.memset(wa_scale_rows[:].bitcast(I32), 0)
+
+        for q in range(4):
+            nc.gpsimd.dma_start(
+                out=wa_scale_rows[32 * q : 32 * q + 4].bitcast(I32),
+                in_=wa_scales[:, 4 * q : 4 * q + 4, :].rearrange("b r n -> r b n").bitcast(I32),
+            )
 
         x_rows = xT.rearrange("(a p i) t -> a i p t", a=PASSES, i=PACK)
         x_plane = {}
@@ -76,6 +82,8 @@ def tile_list_koopman_delay_lift_kernel(tc, xT, wgt, offs, w1, b1, wa_words, wa_
             w1_block[a, b] = load_block(w1_rows[a][:, :, b * W : (b + 1) * W], "w1_%d_%d" % (a, b))
 
         load_x(0, 0)
+        bias = keep.tile([P, PASSES, PACK], F32, name="bias")
+        nc.sync.dma_start(out=bias[:], in_=b1.rearrange("(b p t) -> p b t", b=PASSES, t=PACK))
         for a, i in ((0, 1), (0, 2), (0, 3), (1, 0), (1, 1)):
             load_x(a, i)
         load_w1(0, 0)
@@ -86,8 +94,6 @@ def tile_list_koopman_delay_lift_kernel(tc, xT, wgt, offs, w1, b1, wa_words, wa_
             nc.sync.dma_start(out=w10_half[u][:], in_=w1_rows[1][:, :, u * W // 2 : (u + 1) * W // 2])
             if u == 0:
                 load_x(1, 3)
-        bias = keep.tile([P, PASSES, PACK], F32, name="bias")
-        nc.sync.dma_start(out=bias[:], in_=b1.rearrange("(b p t) -> p b t", b=PASSES, t=PACK))
         load_w1(0, 1)
         load_w1(1, 1)
         wb_rows = wb.rearrange("(b p t) n -> b p t n", b=PASSES, t=PACK)
@@ -95,13 +101,8 @@ def tile_list_koopman_delay_lift_kernel(tc, xT, wgt, offs, w1, b1, wa_words, wa_
         wb_block.append(load_block(wb_rows[1], "wb_1"))
         wa_codes = keep.tile([P, PASSES, 2 * N], U8, name="wa_codes", align_bytes=64)
         nc.sync.dma_start(out=wa_codes[:].bitcast(I32), in_=wa_words.rearrange("b p c -> p b c").bitcast(I32))
-        for q in range(4):
-            nc.sync.dma_start(
-                out=wa_scale_rows[32 * q : 32 * q + 4].bitcast(I32),
-                in_=wa_scales[:, 4 * q : 4 * q + 4, :].rearrange("b r n -> r b n").bitcast(I32),
-            )
 
-        weight = [keep.tile([P, W], F32, name="weight_%d" % h) for h in range(PASSES)]
+        weight = keep.tile([P, S], F32, name="weight")
 
         def turn(n):
             turned = bank(n)
@@ -114,8 +115,7 @@ def tile_list_koopman_delay_lift_kernel(tc, xT, wgt, offs, w1, b1, wa_words, wa_
             back = bank(n)
             for c in range(count):
                 nc.tensor.transpose(back[:, c * P : (c + 1) * P], spread[:, c].rearrange("j g s -> j (g s)"), identity[:])
-            lo = first % PACK * P
-            copy(out=weight[first // PACK][:, lo : lo + count * P], in_=back[:, 0 : count * P])
+            copy(out=weight[:, first * P : (first + count) * P], in_=back[:, 0 : count * P])
 
         for_vector, for_scalar = turn(0), turn(1)
         spread_weight(on_vector, for_vector, 0, 2, 2)
@@ -155,17 +155,18 @@ def tile_list_koopman_delay_lift_kernel(tc, xT, wgt, offs, w1, b1, wa_words, wa_
             nc.vector.quantize_mx(out=codes[:].bitcast(FP8X4), scales=scales[:], in_=src[:].rearrange("p c t -> p (c t)"))
             return codes, scales
 
-        picked = {}
+        picked = [keep.tile([P, PACK, S], F32, name="picked_%d" % a, align_bytes=64) for a in range(PASSES)]
 
         def gather(a, i, h):
-            if i == 0:
-                picked[a, h] = big("picked_%d_%d" % (a, h))
             window = x_plane[a, i][:].indirect(offsets[:, h * LIST_COLUMNS : (h + 1) * LIST_COLUMNS])
-            nc.vector.tensor_tensor(picked[a, h][:, i, :], window, weight[h][:], MULT)
+            columns = slice(h * W, (h + 1) * W)
+            nc.vector.tensor_tensor(picked[a][:, i, columns], window, weight[:, columns], MULT)
 
-        def gather_both_halves(a, i):
-            for h in range(PASSES):
-                gather(a, i, h)
+        def gather_whole(a, i):
+            nc.vector.tensor_tensor(picked[a][:, i, :], x_plane[a, i][:].indirect(offsets[:]), weight[:], MULT)
+
+        def half(a, h):
+            return picked[a][:, :, h * W : (h + 1) * W]
 
         xq, w1q, wbq, zq, sq = {}, {}, {}, {}, {}
 
@@ -226,35 +227,38 @@ def tile_list_koopman_delay_lift_kernel(tc, xT, wgt, offs, w1, b1, wa_words, wa_
         def part(q, lo, hi):
             return q[0][:, lo:hi], q[1][:, lo:hi]
 
-        for i in range(PACK):
-            gather_both_halves(0, i)
-        x0 = woven_tile("x0_woven", 2 * W)
-        for h in range(PASSES):
-            woven_view, plane_view = weave_views(x0[:, h * W : (h + 1) * W, :], picked[0, h][:])
-            on_scalar(out=woven_view, in_=plane_view)
-        gather_both_halves(1, 0)
-        gather_both_halves(1, 1)
-        both = quantise(x0, "xq0", 2 * W, place="x_1_1")
-        for h in range(PASSES):
-            xq[0, h] = part(both, h * W, (h + 1) * W)
+        x01 = woven_tile("s_ring_1")
+        gather(0, 0, 0)
+        gather(0, 0, 1)
+        gather_whole(0, 1)
+        weave_pair(x01, half(0, 1), 0)
+        gather_whole(0, 2)
+        gather(0, 3, 0)
+        x00 = weave(on_scalar, half(0, 0), "s_ring_0")
+        gather(0, 3, 1)
+        weave_pair(x01, half(0, 1), 2)
+        gather_whole(1, 0)
+        xq[0, 0] = quantise(x00, "xq00")
+        gather_whole(1, 1)
+        xq[0, 1] = quantise(x01, "xq01")
         w00 = weave_w1(on_scalar, w1_block[0, 0][:], "s_ring_2")
-        x1 = woven_tile("w1_0_0", 2 * W)
-        x10, x11 = x1[:, 0:W, :], x1[:, W : 2 * W, :]
-        weave_pair(x10, picked[1, 0], 0)
-        weave_pair(x11, picked[1, 1], 0)
-        w10 = woven_tile("v_ring_0")
-        on_scalar(out=w1_woven_view(w10)[:, 0 : P // 2], in_=w1_plane_view(w10_half[0][:]))
-        gather_both_halves(1, 2)
-        w1q[0, 0] = quantise(w00, "w1q00", place="x_1_2")
+        x1 = woven_tile("w1_0_0", S)
+        x10, x11 = x1[:, 0:W, :], x1[:, W:S, :]
+        weave_pair(x10, half(1, 0), 0)
+        weave_pair(x11, half(1, 1), 0)
+        gather_whole(1, 2)
+        w1q[0, 0] = quantise(w00, "w1q00")
         unit00 = open_unit(0, 0, 0)
         unit01 = open_unit(0, 1, 1)
+        w10 = woven_tile("s_ring_0")
+        on_scalar(out=w1_woven_view(w10)[:, 0 : P // 2], in_=w1_plane_view(w10_half[0][:]))
         gather(1, 3, 0)
-        weave_pair(x10, picked[1, 0], 2)
+        weave_pair(x10, half(1, 0), 2)
         gather(1, 3, 1)
-        weave_pair(x11, picked[1, 1], 2)
+        weave_pair(x11, half(1, 1), 2)
         on_vector(out=w1_woven_view(w10)[:, P // 2 : P], in_=w1_plane_view(w10_half[1][:]))
-        xq[1, 0] = quantise(x10, "xq10")
-        w1q[1, 0] = quantise(w10, "w1q10", place="x_0_2")
+        xq[1, 0] = quantise(x10, "xq10", place="x_0_2")
+        w1q[1, 0] = quantise(w10, "w1q10")
         z00 = close_unit(unit00, 0, 0, "x_0_0")
         w01 = weave_w1(on_vector, w1_block[0, 1][:], "v_ring_1")
         xq[1, 1] = quantise(x11, "xq11", place="w1_0_1")
@@ -262,20 +266,20 @@ def tile_list_koopman_delay_lift_kernel(tc, xT, wgt, offs, w1, b1, wa_words, wa_
         w1q[0, 1] = quantise(w01, "w1q01")
         w11 = weave_w1(on_vector, w1_block[1, 1][:], "v_ring_0")
         w1q[1, 1] = quantise(w11, "w1q11")
+        z10 = close_unit(open_unit(1, 0, 0), 1, 0, "x_1_1")
         z00w = weave(on_vector, z00[:], "w1_1_1")
         s00 = weave_square(z00[:], "x_0_2")
-        z10 = close_unit(open_unit(1, 0, 0), 1, 0, "picked_0_0")
+        s10 = weave_square(z10[:], "s_ring_3")
         wb0 = weave(on_vector, wb_block[0][:], "v_ring_1")
         zq[0, 0] = quantise(z00w, "zq00")
         wbq[0] = quantise(wb0, "wbq0")
-        sq[0, 0] = quantise(s00, "sq00")
         wb1 = weave(on_vector, wb_block[1][:], "v_ring_0")
-        wbq[1] = quantise(wb1, "wbq1")
-        s10 = weave_square(z10[:], "s_ring_3")
         z10w = weave(on_vector, z10[:], "wb_1")
+        wbq[1] = quantise(wb1, "wbq1")
+        sq[0, 0] = quantise(s00, "sq00")
         zq[1, 0] = quantise(z10w, "zq10")
-        z01w = weave(on_vector, z01[:], "wb_1")
-        sq[1, 0] = quantise(s10, "sq10", place="picked_0_0")
+        z01w = weave(on_vector, z01[:], "x_0_2")
+        sq[1, 0] = quantise(s10, "sq10", place="x_1_1")
         zq[0, 1] = quantise(z01w, "zq01")
 
         drive_rows = drive.rearrange("(g p) j -> p g j", p=P)
@@ -313,7 +317,7 @@ def tile_list_koopman_delay_lift_kernel(tc, xT, wgt, offs, w1, b1, wa_words, wa_
                 quadratic_pass(y1_view(u, g), b, g, part(codes, 0, Q), b == 1 and g % 2 == 1)
 
         def finish_quarter(u, v):
-            rows = keep.tile([P, 2, Q], F32, name=("wb_0", "picked_0_1", "picked_1_0", "picked_1_1")[2 * u + v], align_bytes=64)
+            rows = keep.tile([P, 2, Q], F32, name=("wb_0", "x_1_2", "picked_0", "picked_1")[2 * u + v], align_bytes=64)
             nc.vector.tensor_tensor(
                 rows[:], y1[u][v][:].rearrange("p (g j) -> p g j", g=2), result[1][:, 2 * v : 2 * v + 2, u * Q : (u + 1) * Q], ADD
             )
@@ -326,7 +330,7 @@ def tile_list_koopman_delay_lift_kernel(tc, xT, wgt, offs, w1, b1, wa_words, wa_
         finish_half0(0)
         linear_quarter(0, 0)
         linear_quarter(0, 1)
-        z11w = weave(on_vector, z11[:], "v_ring_0")
+        z11w = weave(on_vector, z11[:], "s_ring_0")
         finish_half0(1)
         zq[1, 1] = quantise(z11w, "zq11")
         linear_quarter(1, 0)

@@ -57,12 +57,6 @@ def tile_list_koopman_delay_lift_kernel(tc, xT, wgt, offs, w1, b1, wa_words, wa_
         wa_scale_rows = keep.tile([P, PASSES, N], U8, name="wa_scale_rows", align_bytes=64)
         nc.gpsimd.memset(wa_scale_rows[:].bitcast(I32), 0)
 
-        for q in range(4):
-            nc.gpsimd.dma_start(
-                out=wa_scale_rows[32 * q : 32 * q + 4].bitcast(I32),
-                in_=wa_scales[:, 4 * q : 4 * q + 4, :].rearrange("b r n -> r b n").bitcast(I32),
-            )
-
         x_rows = xT.rearrange("(a p i) t -> a i p t", a=PASSES, i=PACK)
         x_plane = {}
 
@@ -88,12 +82,11 @@ def tile_list_koopman_delay_lift_kernel(tc, xT, wgt, offs, w1, b1, wa_words, wa_
             load_x(a, i)
         load_w1(0, 0)
         load_x(1, 2)
+        load_x(1, 3)
         w10_half = []
         for u in range(2):
             w10_half.append(keep.tile([P, PACK, W // 2], F32, name="w1_1_0_%d" % u, align_bytes=64))
             nc.sync.dma_start(out=w10_half[u][:], in_=w1_rows[1][:, :, u * W // 2 : (u + 1) * W // 2])
-            if u == 0:
-                load_x(1, 3)
         load_w1(0, 1)
         load_w1(1, 1)
         wb_rows = wb.rearrange("(b p t) n -> b p t n", b=PASSES, t=PACK)
@@ -101,6 +94,11 @@ def tile_list_koopman_delay_lift_kernel(tc, xT, wgt, offs, w1, b1, wa_words, wa_
         wb_block.append(load_block(wb_rows[1], "wb_1"))
         wa_codes = keep.tile([P, PASSES, 2 * N], U8, name="wa_codes", align_bytes=64)
         nc.sync.dma_start(out=wa_codes[:].bitcast(I32), in_=wa_words.rearrange("b p c -> p b c").bitcast(I32))
+        for q in range(4):
+            nc.sync.dma_start(
+                out=wa_scale_rows[32 * q : 32 * q + 4].bitcast(I32),
+                in_=wa_scales[:, 4 * q : 4 * q + 4, :].rearrange("b r n -> r b n").bitcast(I32),
+            )
 
         weight = keep.tile([P, S], F32, name="weight")
 
@@ -170,7 +168,7 @@ def tile_list_koopman_delay_lift_kernel(tc, xT, wgt, offs, w1, b1, wa_words, wa_
 
         xq, w1q, wbq, zq, sq = {}, {}, {}, {}, {}
 
-        def lift_pass(banks, a, b, h, t):
+        def lift_pass(banks, a, b, h, t, first=0):
             columns = slice(t * P, (t + 1) * P)
             nc.tensor.matmul_mx(
                 out=banks[t][:],
@@ -178,8 +176,8 @@ def tile_list_koopman_delay_lift_kernel(tc, xT, wgt, offs, w1, b1, wa_words, wa_
                 lhsT_scale=w1q[a, b][1][:, columns],
                 rhs=xq[a, h][0][:].bitcast(FP8X4),
                 rhs_scale=xq[a, h][1][:],
-                start=(a == 0),
-                stop=(a == PASSES - 1),
+                start=(a == first),
+                stop=(a != first),
             )
 
         def open_unit(b, h, side):
@@ -192,6 +190,15 @@ def tile_list_koopman_delay_lift_kernel(tc, xT, wgt, offs, w1, b1, wa_words, wa_
             z = big(place)
             for t in range(PACK):
                 lift_pass(banks, 1, b, h, t)
+                nc.scalar.activation(out=z[:, t, :], in_=banks[t][:], func=IDENTITY, bias=bias[:, b, t : t + 1])
+            return z
+
+        def lift_backwards(b, h, side, place):
+            banks = [bank(4 * side + t) for t in range(PACK)]
+            z = big(place)
+            for t in range(PACK):
+                lift_pass(banks, 1, b, h, t, 1)
+                lift_pass(banks, 0, b, h, t, 1)
                 nc.scalar.activation(out=z[:, t, :], in_=banks[t][:], func=IDENTITY, bias=bias[:, b, t : t + 1])
             return z
 
@@ -247,38 +254,37 @@ def tile_list_koopman_delay_lift_kernel(tc, xT, wgt, offs, w1, b1, wa_words, wa_
         weave_pair(x10, half(1, 0), 0)
         weave_pair(x11, half(1, 1), 0)
         gather_whole(1, 2)
-        w1q[0, 0] = quantise(w00, "w1q00")
-        unit00 = open_unit(0, 0, 0)
-        unit01 = open_unit(0, 1, 1)
-        w10 = woven_tile("s_ring_0")
-        on_scalar(out=w1_woven_view(w10)[:, 0 : P // 2], in_=w1_plane_view(w10_half[0][:]))
         gather(1, 3, 0)
         weave_pair(x10, half(1, 0), 2)
         gather(1, 3, 1)
+        w10 = woven_tile("s_ring_0")
+        on_scalar(out=w1_woven_view(w10)[:, 0 : P // 2], in_=w1_plane_view(w10_half[0][:]))
         weave_pair(x11, half(1, 1), 2)
+        w1q[0, 0] = quantise(w00, "w1q00", place="x_1_3")
+        unit00 = open_unit(0, 0, 0)
         on_vector(out=w1_woven_view(w10)[:, P // 2 : P], in_=w1_plane_view(w10_half[1][:]))
-        xq[1, 0] = quantise(x10, "xq10", place="x_0_2")
-        w1q[1, 0] = quantise(w10, "w1q10")
+        xq[1, 0] = quantise(x10, "xq10")
+        w1q[1, 0] = quantise(w10, "w1q10", place="x_0_2")
         z00 = close_unit(unit00, 0, 0, "x_0_0")
         w01 = weave_w1(on_vector, w1_block[0, 1][:], "v_ring_1")
         xq[1, 1] = quantise(x11, "xq11", place="w1_0_1")
-        z01 = close_unit(unit01, 0, 1, "x_0_1")
+        z01 = lift_backwards(0, 1, 1, "x_0_1")
         w1q[0, 1] = quantise(w01, "w1q01")
         w11 = weave_w1(on_vector, w1_block[1, 1][:], "v_ring_0")
         w1q[1, 1] = quantise(w11, "w1q11")
-        z10 = close_unit(open_unit(1, 0, 0), 1, 0, "x_1_1")
         z00w = weave(on_vector, z00[:], "w1_1_1")
         s00 = weave_square(z00[:], "x_0_2")
+        z10 = close_unit(open_unit(1, 0, 0), 1, 0, "x_1_1")
         s10 = weave_square(z10[:], "s_ring_3")
         wb0 = weave(on_vector, wb_block[0][:], "v_ring_1")
         zq[0, 0] = quantise(z00w, "zq00")
         wbq[0] = quantise(wb0, "wbq0")
-        wb1 = weave(on_vector, wb_block[1][:], "v_ring_0")
-        z10w = weave(on_vector, z10[:], "wb_1")
-        wbq[1] = quantise(wb1, "wbq1")
         sq[0, 0] = quantise(s00, "sq00")
+        wb1 = weave(on_vector, wb_block[1][:], "v_ring_0")
+        wbq[1] = quantise(wb1, "wbq1")
+        z10w = weave(on_vector, z10[:], "wb_1")
+        z01w = weave(on_vector, z01[:], "v_ring_0")
         zq[1, 0] = quantise(z10w, "zq10")
-        z01w = weave(on_vector, z01[:], "x_0_2")
         sq[1, 0] = quantise(s10, "sq10", place="x_1_1")
         zq[0, 1] = quantise(z01w, "zq01")
 

@@ -76,8 +76,6 @@ def tile_list_koopman_delay_lift_kernel(tc, xT, wgt, offs, w1, b1, wa_words, wa_
             w1_block[a, b] = load_block(w1_rows[a][:, :, b * W : (b + 1) * W], "w1_%d_%d" % (a, b))
 
         load_x(0, 0)
-        bias = keep.tile([P, PASSES, PACK], F32, name="bias")
-        nc.sync.dma_start(out=bias[:], in_=b1.rearrange("(b p t) -> p b t", b=PASSES, t=PACK))
         for a, i in ((0, 1), (0, 2), (0, 3), (1, 0), (1, 1)):
             load_x(a, i)
         load_w1(0, 0)
@@ -87,6 +85,8 @@ def tile_list_koopman_delay_lift_kernel(tc, xT, wgt, offs, w1, b1, wa_words, wa_
         for u in range(2):
             w10_half.append(keep.tile([P, PACK, W // 2], F32, name="w1_1_0_%d" % u, align_bytes=64))
             nc.sync.dma_start(out=w10_half[u][:], in_=w1_rows[1][:, :, u * W // 2 : (u + 1) * W // 2])
+        bias = keep.tile([P, PASSES, PACK], F32, name="bias")
+        nc.sync.dma_start(out=bias[:], in_=b1.rearrange("(b p t) -> p b t", b=PASSES, t=PACK))
         load_w1(0, 1)
         load_w1(1, 1)
         wb_rows = wb.rearrange("(b p t) n -> b p t n", b=PASSES, t=PACK)
@@ -128,19 +128,20 @@ def tile_list_koopman_delay_lift_kernel(tc, xT, wgt, offs, w1, b1, wa_words, wa_
 
         def weave(copy, src, place):
             dst = woven_tile(place)
-            woven_view, plane_view = weave_views(dst[:], src)
-            copy(out=woven_view, in_=plane_view)
+            copy(
+                out=dst[:].rearrange("p (c u) (s e) -> p c s u e", u=RUN, e=2),
+                in_=src.rearrange("p (s e) (c u) -> p c s u e", u=RUN, e=2),
+            )
             return dst
 
         def weave_pair(dst, src, first):
-            woven_view, plane_view = weave_views(dst[:, :, first : first + 2], src[:, first : first + 2, :])
-            on_scalar(out=woven_view, in_=plane_view)
+            on_scalar(out=dst[:, :, first : first + 2], in_=src[:, first : first + 2, :].rearrange("p e j -> p j e"))
 
         def w1_woven_view(dst):
-            return dst[:].rearrange("p (t m) i -> p m i t", t=PACK)
+            return dst[:].rearrange("p (t m) (s e) -> p m s t e", t=PACK, e=2)
 
         def w1_plane_view(src):
-            return src.rearrange("p i (m t) -> p m i t", t=PACK)
+            return src.rearrange("p (s e) (m t) -> p m s t e", t=PACK, e=2)
 
         def weave_w1(copy, src, place):
             dst = woven_tile(place)
@@ -240,14 +241,13 @@ def tile_list_koopman_delay_lift_kernel(tc, xT, wgt, offs, w1, b1, wa_words, wa_
         gather_whole(0, 1)
         weave_pair(x01, half(0, 1), 0)
         gather_whole(0, 2)
-        gather(0, 3, 0)
+        gather_whole(0, 3)
         x00 = weave(on_scalar, half(0, 0), "s_ring_0")
-        gather(0, 3, 1)
         weave_pair(x01, half(0, 1), 2)
         gather_whole(1, 0)
         xq[0, 0] = quantise(x00, "xq00")
         gather_whole(1, 1)
-        xq[0, 1] = quantise(x01, "xq01")
+        xq[0, 1] = quantise(x01, "xq01", place="x_1_1")
         w00 = weave_w1(on_scalar, w1_block[0, 0][:], "s_ring_2")
         x1 = woven_tile("w1_0_0", S)
         x10, x11 = x1[:, 0:W, :], x1[:, W:S, :]
@@ -274,7 +274,7 @@ def tile_list_koopman_delay_lift_kernel(tc, xT, wgt, offs, w1, b1, wa_words, wa_
         w1q[1, 1] = quantise(w11, "w1q11")
         z00w = weave(on_vector, z00[:], "w1_1_1")
         s00 = weave_square(z00[:], "x_0_2")
-        z10 = close_unit(open_unit(1, 0, 0), 1, 0, "x_1_1")
+        z10 = close_unit(open_unit(1, 0, 0), 1, 0, "w1_1_0_0")
         s10 = weave_square(z10[:], "s_ring_3")
         wb0 = weave(on_vector, wb_block[0][:], "v_ring_1")
         zq[0, 0] = quantise(z00w, "zq00")
@@ -285,7 +285,7 @@ def tile_list_koopman_delay_lift_kernel(tc, xT, wgt, offs, w1, b1, wa_words, wa_
         z10w = weave(on_vector, z10[:], "wb_1")
         z01w = weave(on_vector, z01[:], "v_ring_0")
         zq[1, 0] = quantise(z10w, "zq10")
-        sq[1, 0] = quantise(s10, "sq10", place="x_1_1")
+        sq[1, 0] = quantise(s10, "sq10", place="w1_1_0_0")
         zq[0, 1] = quantise(z01w, "zq01")
 
         drive_rows = drive.rearrange("(g p) j -> p g j", p=P)

@@ -276,16 +276,16 @@ def tile_list_koopman_delay_lift_kernel(tc, xT, wgt, offs, w1, b1, wa_words, wa_
         s00 = weave_square(z00[:], "x_0_2")
         z10 = close_unit(open_unit(1, 0, 0), 1, 0, "w1_1_0_0")
         s10 = weave_square(z10[:], "s_ring_3")
-        wb0 = weave(on_vector, wb_block[0][:], "v_ring_1")
-        zq[0, 0] = quantise(z00w, "zq00")
-        wbq[0] = quantise(wb0, "wbq0")
-        sq[0, 0] = quantise(s00, "sq00")
-        wb1 = weave(on_vector, wb_block[1][:], "v_ring_0")
-        wbq[1] = quantise(wb1, "wbq1")
-        z10w = weave(on_vector, z10[:], "wb_1")
         z01w = weave(on_vector, z01[:], "v_ring_0")
+        zq[0, 0] = quantise(z00w, "zq00")
+        wb0 = weave(on_vector, wb_block[0][:], "v_ring_1")
+        sq[0, 0] = quantise(s00, "sq00")
+        wbq[0] = quantise(wb0, "wbq0")
+        wb1 = weave(on_vector, wb_block[1][:], "s_ring_1")
+        z10w = weave(on_vector, z10[:], "wb_0")
+        wbq[1] = quantise(wb1, "wbq1")
         zq[1, 0] = quantise(z10w, "zq10")
-        sq[1, 0] = quantise(s10, "sq10", place="w1_1_0_0")
+        sq[1, 0] = quantise(s10, "sq10")
         zq[0, 1] = quantise(z01w, "zq01")
 
         drive_rows = drive.rearrange("(g p) j -> p g j", p=P)
@@ -323,7 +323,7 @@ def tile_list_koopman_delay_lift_kernel(tc, xT, wgt, offs, w1, b1, wa_words, wa_
                 quadratic_pass(y1_view(u, g), b, g, part(codes, 0, Q), b == 1 and g % 2 == 1)
 
         def finish_quarter(u, v):
-            rows = keep.tile([P, 2, Q], F32, name=("wb_0", "x_1_2", "picked_0", "picked_1")[2 * u + v], align_bytes=64)
+            rows = keep.tile([P, 2, Q], F32, name=("wb_1", "x_1_2", "picked_0", "picked_1")[2 * u + v], align_bytes=64)
             nc.vector.tensor_tensor(
                 rows[:], y1[u][v][:].rearrange("p (g j) -> p g j", g=2), result[1][:, 2 * v : 2 * v + 2, u * Q : (u + 1) * Q], ADD
             )

@@ -337,17 +337,17 @@ def tile_list_koopman_delay_lift_kernel(tc, xT, wgt, offs, w1, b1, wa_words, wa_
         linear_quarter(0, 0)
         linear_quarter(0, 1)
         z11w = weave(on_vector, z11[:], "s_ring_0")
-        finish_half0(1)
+        quadratic_quarter(0, 0, squares[0, 0])
         zq[1, 1] = quantise(z11w, "zq11")
         linear_quarter(1, 0)
-        quadratic_quarter(0, 0, squares[0, 0])
-        finish_half0(2)
         quadratic_quarter(1, 0, squares[1, 0])
         linear_quarter(1, 1)
-        finish_half0(3)
+        finish_half0(1)
         quadratic_quarter(0, 1, squares[0, 1])
-        finish_quarter(0, 0)
+        finish_half0(2)
+        finish_half0(3)
         quadratic_quarter(1, 1, squares[1, 1])
+        finish_quarter(0, 0)
         finish_quarter(0, 1)
         finish_quarter(1, 0)
         finish_quarter(1, 1)

@@ -85,9 +85,9 @@ def tile_list_koopman_delay_lift_kernel(tc, xT, wgt, offs, w1, b1, wa_words, wa_
         for u in range(2):
             w10_half.append(keep.tile([P, PACK, W // 2], F32, name="w1_1_0_%d" % u, align_bytes=64))
             nc.sync.dma_start(out=w10_half[u][:], in_=w1_rows[1][:, :, u * W // 2 : (u + 1) * W // 2])
+        load_w1(0, 1)
         bias = keep.tile([P, PASSES, PACK], F32, name="bias")
         nc.sync.dma_start(out=bias[:], in_=b1.rearrange("(b p t) -> p b t", b=PASSES, t=PACK))
-        load_w1(0, 1)
         load_w1(1, 1)
         wb_rows = wb.rearrange("(b p t) n -> b p t n", b=PASSES, t=PACK)
         wb_block = [load_block(wb_rows[0], "wb_0")]
@@ -134,8 +134,8 @@ def tile_list_koopman_delay_lift_kernel(tc, xT, wgt, offs, w1, b1, wa_words, wa_
             )
             return dst
 
-        def weave_pair(dst, src, first):
-            on_scalar(out=dst[:, :, first : first + 2], in_=src[:, first : first + 2, :].rearrange("p e j -> p j e"))
+        def weave_pair(dst, src, first, copy=on_scalar):
+            copy(out=dst[:, :, first : first + 2], in_=src[:, first : first + 2, :].rearrange("p e j -> p j e"))
 
         def w1_woven_view(dst):
             return dst[:].rearrange("p (t m) (s e) -> p m s t e", t=PACK, e=2)
@@ -249,25 +249,30 @@ def tile_list_koopman_delay_lift_kernel(tc, xT, wgt, offs, w1, b1, wa_words, wa_
         gather_whole(1, 1)
         xq[0, 1] = quantise(x01, "xq01", place="x_1_1")
         w00 = weave_w1(on_scalar, w1_block[0, 0][:], "s_ring_2")
-        x1 = woven_tile("w1_0_0", S)
-        x10, x11 = x1[:, 0:W, :], x1[:, W:S, :]
+        x10 = woven_tile("w1_0_0")
         weave_pair(x10, half(1, 0), 0)
-        weave_pair(x11, half(1, 1), 0)
         gather_whole(1, 2)
         gather(1, 3, 0)
-        weave_pair(x10, half(1, 0), 2)
         gather(1, 3, 1)
+        weave_pair(x10, half(1, 0), 2, on_vector)
         w10 = woven_tile("s_ring_0")
         on_scalar(out=w1_woven_view(w10)[:, 0 : P // 2], in_=w1_plane_view(w10_half[0][:]))
-        weave_pair(x11, half(1, 1), 2)
+        on_scalar(out=w1_woven_view(w10)[:, P // 2 : P], in_=w1_plane_view(w10_half[1][:]))
+        x11 = weave(on_scalar, half(1, 1), "w1_1_0_1")
         w1q[0, 0] = quantise(w00, "w1q00", place="x_1_3")
-        unit00 = open_unit(0, 0, 0)
-        on_vector(out=w1_woven_view(w10)[:, P // 2 : P], in_=w1_plane_view(w10_half[1][:]))
+        unit00 = [bank(t) for t in range(PACK)]
+        for t in range(3):
+            lift_pass(unit00, 0, 0, 0, t)
         xq[1, 0] = quantise(x10, "xq10")
         w1q[1, 0] = quantise(w10, "w1q10", place="x_0_2")
-        z00 = close_unit(unit00, 0, 0, "x_0_0")
+        z00 = big("x_0_0")
+        for t in range(PACK):
+            lift_pass(unit00, 1, 0, 0, t, t // 3)
+            if t == 3:
+                lift_pass(unit00, 0, 0, 0, t, 1)
+            nc.scalar.activation(out=z00[:, t, :], in_=unit00[t][:], func=IDENTITY, bias=bias[:, 0, t : t + 1])
         w01 = weave_w1(on_vector, w1_block[0, 1][:], "v_ring_1")
-        xq[1, 1] = quantise(x11, "xq11", place="w1_0_1")
+        xq[1, 1] = quantise(x11, "xq11")
         z01 = lift_backwards(0, 1, 1, "x_0_1")
         w1q[0, 1] = quantise(w01, "w1q01")
         w11 = weave_w1(on_vector, w1_block[1, 1][:], "v_ring_0")
@@ -332,7 +337,7 @@ def tile_list_koopman_delay_lift_kernel(tc, xT, wgt, offs, w1, b1, wa_words, wa_
         squares = {}
         for u in range(2):
             for b, z in enumerate((z01, z11)):
-                squares[b, u] = weave_square(z[:, :, u * Q : (u + 1) * Q], (("w1q11_codes", "s_ring_2"), ("w1_0_1", "v_ring_1"))[u][b], Q)
+                squares[b, u] = weave_square(z[:, :, u * Q : (u + 1) * Q], (("w1q11_codes", "s_ring_2"), ("xq11_codes", "v_ring_1"))[u][b], Q)
         finish_half0(0)
         linear_quarter(0, 0)
         linear_quarter(0, 1)

@@ -247,7 +247,6 @@ def tile_list_koopman_delay_lift_kernel(tc, xT, wgt, offs, w1, b1, wa_words, wa_
         gather_whole(1, 0)
         xq[0, 0] = quantise(x00, "xq00")
         gather_whole(1, 1)
-        xq[0, 1] = quantise(x01, "xq01", place="x_1_1")
         w00 = weave_w1(on_scalar, w1_block[0, 0][:], "s_ring_2")
         x10 = woven_tile("w1_0_0")
         weave_pair(x10, half(1, 0), 0)
@@ -273,6 +272,7 @@ def tile_list_koopman_delay_lift_kernel(tc, xT, wgt, offs, w1, b1, wa_words, wa_
             nc.scalar.activation(out=z00[:, t, :], in_=unit00[t][:], func=IDENTITY, bias=bias[:, 0, t : t + 1])
         w01 = weave_w1(on_vector, w1_block[0, 1][:], "v_ring_1")
         xq[1, 1] = quantise(x11, "xq11")
+        xq[0, 1] = quantise(x01, "xq01", place="w1_0_1")
         z01 = lift_backwards(0, 1, 1, "x_0_1")
         w1q[0, 1] = quantise(w01, "w1q01")
         w11 = weave_w1(on_vector, w1_block[1, 1][:], "v_ring_0")
@@ -351,8 +351,8 @@ def tile_list_koopman_delay_lift_kernel(tc, xT, wgt, offs, w1, b1, wa_words, wa_
         quadratic_quarter(0, 1, squares[0, 1])
         finish_half0(2)
         finish_half0(3)
-        quadratic_quarter(1, 1, squares[1, 1])
         finish_quarter(0, 0)
+        quadratic_quarter(1, 1, squares[1, 1])
         finish_quarter(0, 1)
         finish_quarter(1, 0)
         finish_quarter(1, 1)

@@ -78,16 +78,19 @@ def tile_list_koopman_delay_lift_kernel(tc, xT, wgt, offs, w1, b1, wa_words, wa_
         load_x(0, 0)
         for a, i in ((0, 1), (0, 2), (0, 3), (1, 0), (1, 1)):
             load_x(a, i)
-        load_w1(0, 0)
+        EARLY = 3 * W // 4
+        w00_parts = [keep.tile([P, PACK, width], F32, name="w1_0_0_%d" % u, align_bytes=64) for u, width in enumerate((EARLY, W - EARLY))]
+        nc.sync.dma_start(out=w00_parts[0][:], in_=w1_rows[0][:, :, 0:EARLY])
         load_x(1, 2)
         load_x(1, 3)
+        nc.sync.dma_start(out=w00_parts[1][:], in_=w1_rows[0][:, :, EARLY:W])
+        bias = keep.tile([P, PASSES, PACK], F32, name="bias")
+        nc.sync.dma_start(out=bias[:], in_=b1.rearrange("(b p t) -> p b t", b=PASSES, t=PACK))
         w10_half = []
         for u in range(2):
             w10_half.append(keep.tile([P, PACK, W // 2], F32, name="w1_1_0_%d" % u, align_bytes=64))
             nc.sync.dma_start(out=w10_half[u][:], in_=w1_rows[1][:, :, u * W // 2 : (u + 1) * W // 2])
         load_w1(0, 1)
-        bias = keep.tile([P, PASSES, PACK], F32, name="bias")
-        nc.sync.dma_start(out=bias[:], in_=b1.rearrange("(b p t) -> p b t", b=PASSES, t=PACK))
         load_w1(1, 1)
         wb_rows = wb.rearrange("(b p t) n -> b p t n", b=PASSES, t=PACK)
         wb_block = [load_block(wb_rows[0], "wb_0")]
@@ -247,10 +250,12 @@ def tile_list_koopman_delay_lift_kernel(tc, xT, wgt, offs, w1, b1, wa_words, wa_
         gather_whole(1, 0)
         xq[0, 0] = quantise(x00, "xq00")
         gather_whole(1, 1)
-        w00 = weave_w1(on_scalar, w1_block[0, 0][:], "s_ring_2")
-        x10 = woven_tile("w1_0_0")
+        w00 = woven_tile("s_ring_2")
+        on_scalar(out=w1_woven_view(w00)[:, 0 : EARLY // PACK], in_=w1_plane_view(w00_parts[0][:]))
+        x10 = woven_tile("w1_0_0_0")
         weave_pair(x10, half(1, 0), 0)
         gather_whole(1, 2)
+        on_scalar(out=w1_woven_view(w00)[:, EARLY // PACK : P], in_=w1_plane_view(w00_parts[1][:]))
         gather(1, 3, 0)
         gather(1, 3, 1)
         weave_pair(x10, half(1, 0), 2, on_vector)
@@ -260,14 +265,14 @@ def tile_list_koopman_delay_lift_kernel(tc, xT, wgt, offs, w1, b1, wa_words, wa_
         x11 = weave(on_scalar, half(1, 1), "w1_1_0_1")
         w1q[0, 0] = quantise(w00, "w1q00", place="x_1_3")
         unit00 = [bank(t) for t in range(PACK)]
-        for t in range(3):
+        for t in range(2):
             lift_pass(unit00, 0, 0, 0, t)
         xq[1, 0] = quantise(x10, "xq10")
         w1q[1, 0] = quantise(w10, "w1q10", place="x_0_2")
         z00 = big("x_0_0")
         for t in range(PACK):
-            lift_pass(unit00, 1, 0, 0, t, t // 3)
-            if t == 3:
+            lift_pass(unit00, 1, 0, 0, t, t // 2)
+            if t >= 2:
                 lift_pass(unit00, 0, 0, 0, t, 1)
             nc.scalar.activation(out=z00[:, t, :], in_=unit00[t][:], func=IDENTITY, bias=bias[:, 0, t : t + 1])
         w01 = weave_w1(on_vector, w1_block[0, 1][:], "v_ring_1")
@@ -277,7 +282,7 @@ def tile_list_koopman_delay_lift_kernel(tc, xT, wgt, offs, w1, b1, wa_words, wa_
         w1q[0, 1] = quantise(w01, "w1q01")
         w11 = weave_w1(on_vector, w1_block[1, 1][:], "v_ring_0")
         w1q[1, 1] = quantise(w11, "w1q11")
-        z00w = weave(on_vector, z00[:], "w1_1_1")
+        z00w = weave(on_vector, z00[:], "x_1_1")
         s00 = weave_square(z00[:], "x_0_2")
         z10 = close_unit(open_unit(1, 0, 0), 1, 0, "w1_1_0_0")
         s10 = weave_square(z10[:], "s_ring_3")

@@ -84,12 +84,12 @@ def tile_list_koopman_delay_lift_kernel(tc, xT, wgt, offs, w1, b1, wa_words, wa_
         load_x(1, 2)
         load_x(1, 3)
         nc.sync.dma_start(out=w00_parts[1][:], in_=w1_rows[0][:, :, EARLY:W])
-        bias = keep.tile([P, PASSES, PACK], F32, name="bias")
-        nc.sync.dma_start(out=bias[:], in_=b1.rearrange("(b p t) -> p b t", b=PASSES, t=PACK))
         w10_half = []
         for u in range(2):
             w10_half.append(keep.tile([P, PACK, W // 2], F32, name="w1_1_0_%d" % u, align_bytes=64))
             nc.sync.dma_start(out=w10_half[u][:], in_=w1_rows[1][:, :, u * W // 2 : (u + 1) * W // 2])
+        bias = keep.tile([P, PASSES, PACK], F32, name="bias")
+        nc.sync.dma_start(out=bias[:], in_=b1.rearrange("(b p t) -> p b t", b=PASSES, t=PACK))
         load_w1(0, 1)
         load_w1(1, 1)
         wb_rows = wb.rearrange("(b p t) n -> b p t n", b=PASSES, t=PACK)

@@ -90,8 +90,13 @@ def tile_list_koopman_delay_lift_kernel(tc, xT, wgt, offs, w1, b1, wa_words, wa_
             nc.sync.dma_start(out=w10_half[u][:], in_=w1_rows[1][:, :, u * W // 2 : (u + 1) * W // 2])
         bias = keep.tile([P, PASSES, PACK], F32, name="bias")
         nc.sync.dma_start(out=bias[:], in_=b1.rearrange("(b p t) -> p b t", b=PASSES, t=PACK))
-        load_w1(0, 1)
-        load_w1(1, 1)
+        late_cuts = ((0, W // 2, W), (0, EARLY, W))
+        late_part = {}
+        for a in range(PASSES):
+            for u in range(2):
+                lo, hi = late_cuts[a][u : u + 2]
+                late_part[a, u] = keep.tile([P, PACK, hi - lo], F32, name="w1_%d_1_%d" % (a, u), align_bytes=64)
+                nc.sync.dma_start(out=late_part[a, u][:], in_=w1_rows[a][:, :, W + lo : W + hi])
         wb_rows = wb.rearrange("(b p t) n -> b p t n", b=PASSES, t=PACK)
         wb_block = [load_block(wb_rows[0], "wb_0")]
         wb_block.append(load_block(wb_rows[1], "wb_1"))
@@ -149,6 +154,13 @@ def tile_list_koopman_delay_lift_kernel(tc, xT, wgt, offs, w1, b1, wa_words, wa_
         def weave_w1(copy, src, place):
             dst = woven_tile(place)
             copy(out=w1_woven_view(dst), in_=w1_plane_view(src))
+            return dst
+
+        def weave_late(a, place):
+            dst = woven_tile(place)
+            for u in range(2):
+                lo, hi = late_cuts[a][u : u + 2]
+                on_vector(out=w1_woven_view(dst)[:, lo // PACK : hi // PACK], in_=w1_plane_view(late_part[a, u][:]))
             return dst
 
         def quantise(src, name, width=W, place=None):
@@ -275,12 +287,12 @@ def tile_list_koopman_delay_lift_kernel(tc, xT, wgt, offs, w1, b1, wa_words, wa_
             if t >= 2:
                 lift_pass(unit00, 0, 0, 0, t, 1)
             nc.scalar.activation(out=z00[:, t, :], in_=unit00[t][:], func=IDENTITY, bias=bias[:, 0, t : t + 1])
-        w01 = weave_w1(on_vector, w1_block[0, 1][:], "v_ring_1")
+        w01 = weave_late(0, "v_ring_1")
         xq[1, 1] = quantise(x11, "xq11")
-        xq[0, 1] = quantise(x01, "xq01", place="w1_0_1")
+        xq[0, 1] = quantise(x01, "xq01", place="w1_0_1_1")
         z01 = lift_backwards(0, 1, 1, "x_0_1")
         w1q[0, 1] = quantise(w01, "w1q01")
-        w11 = weave_w1(on_vector, w1_block[1, 1][:], "v_ring_0")
+        w11 = weave_late(1, "v_ring_0")
         w1q[1, 1] = quantise(w11, "w1q11")
         z00w = weave(on_vector, z00[:], "x_1_1")
         s00 = weave_square(z00[:], "x_0_2")

@@ -23,11 +23,12 @@ P = 128
 PACK = 4
 PASSES = 2
 W = 512
+Q = W // 2
 GROUPS = N // P
 RUN = 4
-LIST_COLUMNS = W // 16
 HEADS = 8
 SHARE = P // HEADS
+EARLY = 3 * W // 4
 
 
 def tile_list_koopman_delay_lift_kernel(tc, xT, wgt, offs, w1, b1, wa_words, wa_scales, wb, drive, out):
@@ -40,67 +41,57 @@ def tile_list_koopman_delay_lift_kernel(tc, xT, wgt, offs, w1, b1, wa_words, wa_
         def bank(n):
             return psum.tile([P, W], F32, name="bank_%d" % n)
 
-        def big(place):
-            return keep.tile([P, PACK, W], F32, name=place, align_bytes=64)
+        def at(place, shape, dtype=F32):
+            return keep.tile(shape, dtype, name=place, align_bytes=64)
 
-        wgt_rows = keep.tile([P, P], F32, name="wgt_rows")
-        nc.sync.dma_start(
-            out=wgt_rows[:],
-            in_=wgt.rearrange("(g s) j -> g (s j)", s=SHARE)[:, 0 : SHARE * P].rearrange("g (u j) -> g u j", j=P),
+        def load(place, shape, src):
+            tile = at(place, shape)
+            nc.sync.dma_start(out=tile[:], in_=src)
+            return tile
+
+        wgt_rows = load(
+            "wgt_rows",
+            [P, P],
+            wgt.rearrange("(g s) j -> g (s j)", s=SHARE)[:, 0 : SHARE * P].rearrange("g (u j) -> g u j", j=P),
         )
         offsets = keep.tile([P, S // 16], U16, name="offsets")
         nc.sync.dma_start(offsets[:], offs)
-
-        identity = keep.tile([P, P], F32, name="identity")
+        identity = at("identity", [P, P])
         make_identity(nc, identity[:])
-
-        wa_scale_rows = keep.tile([P, PASSES, N], U8, name="wa_scale_rows", align_bytes=64)
+        wa_scale_rows = at("wa_scale_rows", [P, PASSES, N], U8)
         nc.gpsimd.memset(wa_scale_rows[:].bitcast(I32), 0)
 
         x_rows = xT.rearrange("(a p i) t -> a i p t", a=PASSES, i=PACK)
-        x_plane = {}
+        w1_rows = w1.rearrange("(a p i) r -> a p i r", a=PASSES, i=PACK)
+        x_plane, w1_part = {}, {}
+        cut = {(0, 0): EARLY, (1, 0): Q, (0, 1): Q, (1, 1): EARLY}
 
         def load_x(a, i):
-            x_plane[a, i] = keep.tile([P, T], F32, name="x_%d_%d" % (a, i), align_bytes=64)
-            nc.sync.dma_start(out=x_plane[a, i][:], in_=x_rows[a, i])
+            x_plane[a, i] = load("x_%d_%d" % (a, i), [P, T], x_rows[a, i])
 
-        def load_block(src, place):
-            block = big(place)
-            nc.sync.dma_start(out=block[:], in_=src)
-            return block
+        def part_range(a, b, u):
+            return (0, cut[a, b], W)[u : u + 2]
 
-        w1_rows = w1.rearrange("(a p i) r -> a p i r", a=PASSES, i=PACK)
-        w1_block = {}
+        def load_w1(a, b, u):
+            lo, hi = part_range(a, b, u)
+            w1_part[a, b, u] = load("w1_%d_%d_%d" % (a, b, u), [P, PACK, hi - lo], w1_rows[a][:, :, b * W + lo : b * W + hi])
 
-        def load_w1(a, b):
-            w1_block[a, b] = load_block(w1_rows[a][:, :, b * W : (b + 1) * W], "w1_%d_%d" % (a, b))
-
-        load_x(0, 0)
-        for a, i in ((0, 1), (0, 2), (0, 3), (1, 0), (1, 1)):
-            load_x(a, i)
-        EARLY = 3 * W // 4
-        w00_parts = [keep.tile([P, PACK, width], F32, name="w1_0_0_%d" % u, align_bytes=64) for u, width in enumerate((EARLY, W - EARLY))]
-        nc.sync.dma_start(out=w00_parts[0][:], in_=w1_rows[0][:, :, 0:EARLY])
+        for n in range(6):
+            load_x(n // PACK, n % PACK)
+        load_w1(0, 0, 0)
         load_x(1, 2)
         load_x(1, 3)
-        nc.sync.dma_start(out=w00_parts[1][:], in_=w1_rows[0][:, :, EARLY:W])
-        w10_half = []
-        for u in range(2):
-            w10_half.append(keep.tile([P, PACK, W // 2], F32, name="w1_1_0_%d" % u, align_bytes=64))
-            nc.sync.dma_start(out=w10_half[u][:], in_=w1_rows[1][:, :, u * W // 2 : (u + 1) * W // 2])
-        bias = keep.tile([P, PASSES, PACK], F32, name="bias")
-        nc.sync.dma_start(out=bias[:], in_=b1.rearrange("(b p t) -> p b t", b=PASSES, t=PACK))
-        late_cuts = ((0, W // 2, W), (0, EARLY, W))
-        late_part = {}
-        for a in range(PASSES):
-            for u in range(2):
-                lo, hi = late_cuts[a][u : u + 2]
-                late_part[a, u] = keep.tile([P, PACK, hi - lo], F32, name="w1_%d_1_%d" % (a, u), align_bytes=64)
-                nc.sync.dma_start(out=late_part[a, u][:], in_=w1_rows[a][:, :, W + lo : W + hi])
+        load_w1(0, 0, 1)
+        load_w1(1, 0, 0)
+        load_w1(1, 0, 1)
+        bias = load("bias", [P, PASSES, PACK], b1.rearrange("(b p t) -> p b t", b=PASSES, t=PACK))
+        load_w1(0, 1, 0)
+        load_w1(0, 1, 1)
+        load_w1(1, 1, 0)
+        load_w1(1, 1, 1)
         wb_rows = wb.rearrange("(b p t) n -> b p t n", b=PASSES, t=PACK)
-        wb_block = [load_block(wb_rows[0], "wb_0")]
-        wb_block.append(load_block(wb_rows[1], "wb_1"))
-        wa_codes = keep.tile([P, PASSES, 2 * N], U8, name="wa_codes", align_bytes=64)
+        wb_block = [load("wb_%d" % b, [P, PACK, W], wb_rows[b]) for b in range(PASSES)]
+        wa_codes = at("wa_codes", [P, PASSES, 2 * N], U8)
         nc.sync.dma_start(out=wa_codes[:].bitcast(I32), in_=wa_words.rearrange("b p c -> p b c").bitcast(I32))
         for q in range(4):
             nc.sync.dma_start(
@@ -108,7 +99,7 @@ def tile_list_koopman_delay_lift_kernel(tc, xT, wgt, offs, w1, b1, wa_words, wa_
                 in_=wa_scales[:, 4 * q : 4 * q + 4, :].rearrange("b r n -> r b n").bitcast(I32),
             )
 
-        weight = keep.tile([P, S], F32, name="weight")
+        weight = at("weight", [P, S])
 
         def turn(n):
             turned = bank(n)
@@ -116,7 +107,7 @@ def tile_list_koopman_delay_lift_kernel(tc, xT, wgt, offs, w1, b1, wa_words, wa_
             return turned[:, 0:P].rearrange("j (g u) -> j u g", u=SHARE)
 
         def spread_weight(copy, by_head, first, count, n):
-            spread = keep.tile([P, count, HEADS, SHARE], F32, name="spread_%d" % first)
+            spread = at("spread_%d" % first, [P, count, HEADS, SHARE])
             copy(out=spread[:], in_=by_head[:, first : first + count, :].unsqueeze(3).to_broadcast([P, count, HEADS, SHARE]))
             back = bank(n)
             for c in range(count):
@@ -129,10 +120,7 @@ def tile_list_koopman_delay_lift_kernel(tc, xT, wgt, offs, w1, b1, wa_words, wa_
         spread_weight(on_scalar, for_scalar, 4, 4, 4)
 
         def woven_tile(place, width=W):
-            return keep.tile([P, width, PACK], BF16, name=place, align_bytes=64)
-
-        def weave_views(dst, src):
-            return dst.rearrange("p (c u) t -> p c t u", u=RUN), src.rearrange("p t (c u) -> p c t u", u=RUN)
+            return at(place, [P, width, PACK], BF16)
 
         def weave(copy, src, place):
             dst = woven_tile(place)
@@ -142,166 +130,129 @@ def tile_list_koopman_delay_lift_kernel(tc, xT, wgt, offs, w1, b1, wa_words, wa_
             )
             return dst
 
-        def weave_pair(dst, src, first, copy=on_scalar):
+        def weave_pair(copy, dst, src, first):
             copy(out=dst[:, :, first : first + 2], in_=src[:, first : first + 2, :].rearrange("p e j -> p j e"))
 
-        def w1_woven_view(dst):
-            return dst[:].rearrange("p (t m) (s e) -> p m s t e", t=PACK, e=2)
+        def weave_w1(copy, dst, a, b, u):
+            lo, hi = part_range(a, b, u)
+            copy(
+                out=dst[:].rearrange("p (t m) (s e) -> p m s t e", t=PACK, e=2)[:, lo // PACK : hi // PACK],
+                in_=w1_part[a, b, u][:].rearrange("p (s e) (m t) -> p m s t e", t=PACK, e=2),
+            )
 
-        def w1_plane_view(src):
-            return src.rearrange("p (s e) (m t) -> p m s t e", t=PACK, e=2)
-
-        def weave_w1(copy, src, place):
-            dst = woven_tile(place)
-            copy(out=w1_woven_view(dst), in_=w1_plane_view(src))
-            return dst
-
-        def weave_late(a, place):
-            dst = woven_tile(place)
-            for u in range(2):
-                lo, hi = late_cuts[a][u : u + 2]
-                on_vector(out=w1_woven_view(dst)[:, lo // PACK : hi // PACK], in_=w1_plane_view(late_part[a, u][:]))
+        def weave_square(z, place, width=W):
+            dst = woven_tile(place, width)
+            nc.scalar.activation(
+                out=dst[:].rearrange("p (c u) t -> p c t u", u=RUN), in_=z.rearrange("p t (c u) -> p c t u", u=RUN), func=SQUARE
+            )
             return dst
 
         def quantise(src, name, width=W, place=None):
-            codes = keep.tile([P, width], U32, name=place or name + "_codes", align_bytes=64)
-            scales = keep.tile([P, width], U8, name=name + "_scales", align_bytes=64)
+            codes = at(place or name + "_codes", [P, width], U32)
+            scales = at(name + "_scales", [P, width], U8)
             nc.vector.quantize_mx(out=codes[:].bitcast(FP8X4), scales=scales[:], in_=src[:].rearrange("p c t -> p (c t)"))
             return codes, scales
 
-        picked = [keep.tile([P, PACK, S], F32, name="picked_%d" % a, align_bytes=64) for a in range(PASSES)]
+        picked = [at("picked_%d" % a, [P, PACK, S]) for a in range(PASSES)]
 
-        def gather(a, i, h):
-            window = x_plane[a, i][:].indirect(offsets[:, h * LIST_COLUMNS : (h + 1) * LIST_COLUMNS])
-            columns = slice(h * W, (h + 1) * W)
-            nc.vector.tensor_tensor(picked[a][:, i, columns], window, weight[:, columns], MULT)
-
-        def gather_whole(a, i):
-            nc.vector.tensor_tensor(picked[a][:, i, :], x_plane[a, i][:].indirect(offsets[:]), weight[:], MULT)
+        def gather(a, i, lo=0, hi=S):
+            window = x_plane[a, i][:].indirect(offsets[:, lo // 16 : hi // 16])
+            nc.vector.tensor_tensor(picked[a][:, i, lo:hi], window, weight[:, lo:hi], MULT)
 
         def half(a, h):
             return picked[a][:, :, h * W : (h + 1) * W]
 
-        xq, w1q, wbq, zq, sq = {}, {}, {}, {}, {}
-
-        def lift_pass(banks, a, b, h, t, first=0):
-            columns = slice(t * P, (t + 1) * P)
+        def mx_pass(y, left, left_scales, right, start, stop):
             nc.tensor.matmul_mx(
-                out=banks[t][:],
-                lhsT=w1q[a, b][0][:, columns].bitcast(FP8X4),
-                lhsT_scale=w1q[a, b][1][:, columns],
-                rhs=xq[a, h][0][:].bitcast(FP8X4),
-                rhs_scale=xq[a, h][1][:],
-                start=(a == first),
-                stop=(a != first),
-            )
-
-        def open_unit(b, h, side):
-            banks = [bank(4 * side + t) for t in range(PACK)]
-            for t in range(PACK):
-                lift_pass(banks, 0, b, h, t)
-            return banks
-
-        def close_unit(banks, b, h, place):
-            z = big(place)
-            for t in range(PACK):
-                lift_pass(banks, 1, b, h, t)
-                nc.scalar.activation(out=z[:, t, :], in_=banks[t][:], func=IDENTITY, bias=bias[:, b, t : t + 1])
-            return z
-
-        def lift_backwards(b, h, side, place):
-            banks = [bank(4 * side + t) for t in range(PACK)]
-            z = big(place)
-            for t in range(PACK):
-                lift_pass(banks, 1, b, h, t, 1)
-                lift_pass(banks, 0, b, h, t, 1)
-                nc.scalar.activation(out=z[:, t, :], in_=banks[t][:], func=IDENTITY, bias=bias[:, b, t : t + 1])
-            return z
-
-        def weave_square(z, place, width=W):
-            dst = woven_tile(place, width)
-            woven_view, plane_view = weave_views(dst[:], z)
-            nc.scalar.activation(out=woven_view, in_=plane_view, func=SQUARE)
-            return dst
-
-        def linear_pass(y, b, g, z, start):
-            nc.tensor.matmul_mx(
-                out=y,
-                lhsT=wa_codes[:, b, 2 * g * P : 2 * (g + 1) * P].bitcast(FP4X4),
-                lhsT_scale=wa_scale_rows[:, b, g * P : (g + 1) * P],
-                rhs=z[0].bitcast(FP8X4),
-                rhs_scale=z[1],
-                start=start,
-                stop=False,
-            )
-
-        def quadratic_pass(y, b, g, s, stop):
-            columns = slice(g * P, (g + 1) * P)
-            nc.tensor.matmul_mx(
-                out=y,
-                lhsT=wbq[b][0][:, columns].bitcast(FP8X4),
-                lhsT_scale=wbq[b][1][:, columns],
-                rhs=s[0].bitcast(FP8X4),
-                rhs_scale=s[1],
-                start=False,
-                stop=stop,
+                out=y, lhsT=left, lhsT_scale=left_scales, rhs=right[0].bitcast(FP8X4), rhs_scale=right[1], start=start, stop=stop
             )
 
         def part(q, lo, hi):
             return q[0][:, lo:hi], q[1][:, lo:hi]
 
+        xq, w1q, wbq, zq, sq = {}, {}, {}, {}, {}
+
+        def lift_pass(banks, a, b, h, t, first):
+            codes, scales = part(w1q[a, b], t * P, (t + 1) * P)
+            mx_pass(banks[t][:], codes.bitcast(FP8X4), scales, part(xq[a, h], 0, W), a == first, a != first)
+
+        def lift(b, h, side, place, opened, first):
+            banks = [bank(PACK * side + t) for t in range(PACK)]
+            for t in range(opened):
+                lift_pass(banks, first, b, h, t, first)
+            return banks, b, h, place, opened, first
+
+        def close(banks, b, h, place, opened, first):
+            z = at(place, [P, PACK, W])
+            for t in range(PACK):
+                if t < opened:
+                    lift_pass(banks, 1 - first, b, h, t, first)
+                else:
+                    lift_pass(banks, 1 - first, b, h, t, 1 - first)
+                    lift_pass(banks, first, b, h, t, 1 - first)
+                nc.scalar.activation(out=z[:, t, :], in_=banks[t][:], func=IDENTITY, bias=bias[:, b, t : t + 1])
+            return z
+
+        def linear_pass(y, b, g, z, start):
+            left = wa_codes[:, b, 2 * g * P : 2 * (g + 1) * P].bitcast(FP4X4)
+            mx_pass(y, left, wa_scale_rows[:, b, g * P : (g + 1) * P], z, start, False)
+
+        def quadratic_pass(y, b, g, s, stop):
+            codes, scales = part(wbq[b], g * P, (g + 1) * P)
+            mx_pass(y, codes.bitcast(FP8X4), scales, s, False, stop)
+
         x01 = woven_tile("s_ring_1")
-        gather(0, 0, 0)
-        gather(0, 0, 1)
-        gather_whole(0, 1)
-        weave_pair(x01, half(0, 1), 0)
-        gather_whole(0, 2)
-        gather_whole(0, 3)
+        gather(0, 0, 0, W)
+        gather(0, 0, W, S)
+        gather(0, 1)
+        weave_pair(on_scalar, x01, half(0, 1), 0)
+        gather(0, 2)
+        gather(0, 3)
         x00 = weave(on_scalar, half(0, 0), "s_ring_0")
-        weave_pair(x01, half(0, 1), 2)
-        gather_whole(1, 0)
+        weave_pair(on_scalar, x01, half(0, 1), 2)
+        gather(1, 0)
         xq[0, 0] = quantise(x00, "xq00")
-        gather_whole(1, 1)
+        gather(1, 1)
         w00 = woven_tile("s_ring_2")
-        on_scalar(out=w1_woven_view(w00)[:, 0 : EARLY // PACK], in_=w1_plane_view(w00_parts[0][:]))
+        weave_w1(on_scalar, w00, 0, 0, 0)
         x10 = woven_tile("w1_0_0_0")
-        weave_pair(x10, half(1, 0), 0)
-        gather_whole(1, 2)
-        on_scalar(out=w1_woven_view(w00)[:, EARLY // PACK : P], in_=w1_plane_view(w00_parts[1][:]))
-        gather(1, 3, 0)
-        gather(1, 3, 1)
-        weave_pair(x10, half(1, 0), 2, on_vector)
+        weave_pair(on_scalar, x10, half(1, 0), 0)
+        gather(1, 2)
+        weave_w1(on_scalar, w00, 0, 0, 1)
+        gather(1, 3, 0, W)
+        gather(1, 3, W, S)
+        weave_pair(on_vector, x10, half(1, 0), 2)
         w10 = woven_tile("s_ring_0")
-        on_scalar(out=w1_woven_view(w10)[:, 0 : P // 2], in_=w1_plane_view(w10_half[0][:]))
-        on_scalar(out=w1_woven_view(w10)[:, P // 2 : P], in_=w1_plane_view(w10_half[1][:]))
-        x11 = weave(on_scalar, half(1, 1), "w1_1_0_1")
+        weave_w1(on_scalar, w10, 1, 0, 0)
+        weave_w1(on_scalar, w10, 1, 0, 1)
+        w01 = woven_tile("v_ring_1")
+        weave_w1(on_scalar, w01, 0, 1, 0)
         w1q[0, 0] = quantise(w00, "w1q00", place="x_1_3")
-        unit00 = [bank(t) for t in range(PACK)]
-        for t in range(2):
-            lift_pass(unit00, 0, 0, 0, t)
+        unit00 = lift(0, 0, 0, "w1_0_1_0", 2, 0)
         xq[1, 0] = quantise(x10, "xq10")
         w1q[1, 0] = quantise(w10, "w1q10", place="x_0_2")
-        z00 = big("x_0_0")
-        for t in range(PACK):
-            lift_pass(unit00, 1, 0, 0, t, t // 2)
-            if t >= 2:
-                lift_pass(unit00, 0, 0, 0, t, 1)
-            nc.scalar.activation(out=z00[:, t, :], in_=unit00[t][:], func=IDENTITY, bias=bias[:, 0, t : t + 1])
-        w01 = weave_late(0, "v_ring_1")
+        z00 = close(*unit00)
+
+        x11 = weave(on_vector, half(1, 1), "s_ring_0")
+        weave_w1(on_vector, w01, 0, 1, 1)
         xq[1, 1] = quantise(x11, "xq11")
+        unit01 = lift(0, 1, 1, "x_0_1", PACK, 1)
         xq[0, 1] = quantise(x01, "xq01", place="w1_0_1_1")
-        z01 = lift_backwards(0, 1, 1, "x_0_1")
         w1q[0, 1] = quantise(w01, "w1q01")
-        w11 = weave_late(1, "v_ring_0")
-        w1q[1, 1] = quantise(w11, "w1q11")
+        s00 = weave_square(z00[:], "x_0_0")
+        z01 = close(*unit01)
+        unit10 = lift(1, 0, 0, "w1_1_0_0", PACK, 0)
+        w11 = woven_tile("v_ring_0")
+        weave_w1(on_vector, w11, 1, 1, 0)
+        weave_w1(on_vector, w11, 1, 1, 1)
         z00w = weave(on_vector, z00[:], "x_1_1")
-        s00 = weave_square(z00[:], "x_0_2")
-        z10 = close_unit(open_unit(1, 0, 0), 1, 0, "w1_1_0_0")
+        w1q[1, 1] = quantise(w11, "w1q11")
+        z10 = close(*unit10)
         s10 = weave_square(z10[:], "s_ring_3")
-        z01w = weave(on_vector, z01[:], "v_ring_0")
         zq[0, 0] = quantise(z00w, "zq00")
         wb0 = weave(on_vector, wb_block[0][:], "v_ring_1")
         sq[0, 0] = quantise(s00, "sq00")
+        z01w = weave(on_vector, z01[:], "v_ring_0")
         wbq[0] = quantise(wb0, "wbq0")
         wb1 = weave(on_vector, wb_block[1][:], "s_ring_1")
         z10w = weave(on_vector, z10[:], "wb_0")
@@ -312,24 +263,23 @@ def tile_list_koopman_delay_lift_kernel(tc, xT, wgt, offs, w1, b1, wa_words, wa_
 
         drive_rows = drive.rearrange("(g p) j -> p g j", p=P)
         out_rows = out.rearrange("(g p) j -> p g j", p=P)
-        result = [load_block(drive_rows[:, :, h * W : (h + 1) * W], ("x_1_0", "x_1_3")[h]) for h in range(PASSES)]
+        given = [load(("x_1_0", "x_1_3")[h], [P, GROUPS, W], drive_rows[:, :, h * W : (h + 1) * W]) for h in range(2)]
 
-        y0 = [bank(4 + g) for g in range(GROUPS)]
+        y0 = [bank(PACK + g) for g in range(GROUPS)]
         for g in range(GROUPS):
             linear_pass(y0[g][:], 0, g, part(zq[0, 0], 0, W), True)
         for g in range(GROUPS):
             quadratic_pass(y0[g][:], 0, g, part(sq[0, 0], 0, W), False)
-        z11 = close_unit(open_unit(1, 1, 0), 1, 1, "x_0_3")
+        z11 = close(*lift(1, 1, 0, "x_0_3", PACK, 0))
         for g in range(GROUPS):
             linear_pass(y0[g][:], 1, g, part(zq[1, 0], 0, W), False)
         for g in range(GROUPS):
             quadratic_pass(y0[g][:], 1, g, part(sq[1, 0], 0, W), True)
 
         def finish_half0(g):
-            nc.vector.tensor_tensor(result[0][:, g, :], y0[g][:], result[0][:, g, :], ADD)
-            nc.sync.dma_start(out=out_rows[:, g, 0:W], in_=result[0][:, g, :])
+            nc.vector.tensor_tensor(given[0][:, g, :], y0[g][:], given[0][:, g, :], ADD)
+            nc.sync.dma_start(out=out_rows[:, g, 0:W], in_=given[0][:, g, :])
 
-        Q = W // 2
         y1 = [[bank(2 * u + v) for v in range(2)] for u in range(2)]
 
         def y1_view(u, g):
@@ -345,16 +295,17 @@ def tile_list_koopman_delay_lift_kernel(tc, xT, wgt, offs, w1, b1, wa_words, wa_
                 quadratic_pass(y1_view(u, g), b, g, part(codes, 0, Q), b == 1 and g % 2 == 1)
 
         def finish_quarter(u, v):
-            rows = keep.tile([P, 2, Q], F32, name=("wb_1", "x_1_2", "picked_0", "picked_1")[2 * u + v], align_bytes=64)
+            rows = at(("wb_1", "x_1_2", "picked_0", "picked_1")[2 * u + v], [P, 2, Q])
             nc.vector.tensor_tensor(
-                rows[:], y1[u][v][:].rearrange("p (g j) -> p g j", g=2), result[1][:, 2 * v : 2 * v + 2, u * Q : (u + 1) * Q], ADD
+                rows[:], y1[u][v][:].rearrange("p (g j) -> p g j", g=2), given[1][:, 2 * v : 2 * v + 2, u * Q : (u + 1) * Q], ADD
             )
             nc.sync.dma_start(out=out_rows[:, 2 * v : 2 * v + 2, W + u * Q : W + (u + 1) * Q], in_=rows[:])
 
-        squares = {}
-        for u in range(2):
-            for b, z in enumerate((z01, z11)):
-                squares[b, u] = weave_square(z[:, :, u * Q : (u + 1) * Q], (("w1q11_codes", "s_ring_2"), ("xq11_codes", "v_ring_1"))[u][b], Q)
+        def square_quarter(b, u):
+            place = (("w1q11_codes", "s_ring_2"), ("xq11_codes", "v_ring_1"))[u][b]
+            return weave_square((z01, z11)[b][:, :, u * Q : (u + 1) * Q], place, Q)
+
+        squares = {(b, u): square_quarter(b, u) for u in range(2) for b in range(PASSES)}
         finish_half0(0)
         linear_quarter(0, 0)
         linear_quarter(0, 1)

@@ -225,23 +225,23 @@ def tile_list_koopman_delay_lift_kernel(tc, xT, wgt, offs, w1, b1, wa_words, wa_
         w10 = woven_tile("s_ring_0")
         weave_w1(on_scalar, w10, 1, 0, 0)
         weave_w1(on_scalar, w10, 1, 0, 1)
-        w01 = woven_tile("v_ring_1")
-        weave_w1(on_scalar, w01, 0, 1, 0)
+        x11 = weave(on_scalar, half(1, 1), "w1_1_0_1")
         w1q[0, 0] = quantise(w00, "w1q00", place="x_1_3")
-        unit00 = lift(0, 0, 0, "w1_0_1_0", 2, 0)
+        unit00 = lift(0, 0, 0, "picked_0", 2, 0)
         xq[1, 0] = quantise(x10, "xq10")
         w1q[1, 0] = quantise(w10, "w1q10", place="x_0_2")
         z00 = close(*unit00)
 
-        x11 = weave(on_vector, half(1, 1), "s_ring_0")
+        xq[0, 1] = quantise(x01, "xq01", place="w1_1_0_0")
+        w01 = woven_tile("v_ring_1")
+        weave_w1(on_vector, w01, 0, 1, 0)
         weave_w1(on_vector, w01, 0, 1, 1)
         xq[1, 1] = quantise(x11, "xq11")
-        unit01 = lift(0, 1, 1, "x_0_1", PACK, 1)
-        xq[0, 1] = quantise(x01, "xq01", place="w1_0_1_1")
+        unit01 = lift(0, 1, 1, "x_0_1", 0, 0)
         w1q[0, 1] = quantise(w01, "w1q01")
         s00 = weave_square(z00[:], "x_0_0")
         z01 = close(*unit01)
-        unit10 = lift(1, 0, 0, "w1_1_0_0", PACK, 0)
+        unit10 = lift(1, 0, 0, "x_1_2", PACK, 0)
         w11 = woven_tile("v_ring_0")
         weave_w1(on_vector, w11, 1, 1, 0)
         weave_w1(on_vector, w11, 1, 1, 1)

@@ -64,13 +64,13 @@ def tile_list_koopman_delay_lift_kernel(tc, xT, wgt, offs, w1, b1, wa_words, wa_
         x_rows = xT.rearrange("(a p i) t -> a i p t", a=PASSES, i=PACK)
         w1_rows = w1.rearrange("(a p i) r -> a p i r", a=PASSES, i=PACK)
         x_plane, w1_part = {}, {}
-        cut = {(0, 0): EARLY, (1, 0): Q, (0, 1): Q, (1, 1): EARLY}
+        cuts = {(0, 0): (0, EARLY, W), (1, 0): (0, Q, EARLY, W), (0, 1): (0, Q, W), (1, 1): (0, EARLY, W)}
 
         def load_x(a, i):
             x_plane[a, i] = load("x_%d_%d" % (a, i), [P, T], x_rows[a, i])
 
         def part_range(a, b, u):
-            return (0, cut[a, b], W)[u : u + 2]
+            return cuts[a, b][u : u + 2]
 
         def load_w1(a, b, u):
             lo, hi = part_range(a, b, u)
@@ -84,6 +84,7 @@ def tile_list_koopman_delay_lift_kernel(tc, xT, wgt, offs, w1, b1, wa_words, wa_
         load_w1(0, 0, 1)
         load_w1(1, 0, 0)
         load_w1(1, 0, 1)
+        load_w1(1, 0, 2)
         bias = load("bias", [P, PASSES, PACK], b1.rearrange("(b p t) -> p b t", b=PASSES, t=PACK))
         load_w1(0, 1, 0)
         load_w1(0, 1, 1)
@@ -225,7 +226,8 @@ def tile_list_koopman_delay_lift_kernel(tc, xT, wgt, offs, w1, b1, wa_words, wa_
         w10 = woven_tile("s_ring_0")
         weave_w1(on_scalar, w10, 1, 0, 0)
         weave_w1(on_scalar, w10, 1, 0, 1)
-        x11 = weave(on_scalar, half(1, 1), "w1_1_0_1")
+        weave_w1(on_scalar, w10, 1, 0, 2)
+        x11 = weave(on_scalar, half(1, 1), "w1_1_0_2")
         w1q[0, 0] = quantise(w00, "w1q00", place="x_1_3")
         unit00 = lift(0, 0, 0, "picked_0", 2, 0)
         xq[1, 0] = quantise(x10, "xq10")

@@ -52,7 +52,7 @@ def tile_list_koopman_delay_lift_kernel(tc, xT, wgt, offs, w1, b1, wa_words, wa_
         wgt_rows = load(
             "wgt_rows",
             [P, P],
-            wgt.rearrange("(g s) j -> g (s j)", s=SHARE)[:, 0 : SHARE * P].rearrange("g (u j) -> g u j", j=P),
+            wgt.rearrange("(n r) (u j) -> n r u j", r=S // P, j=P)[:, 0],
         )
         offsets = keep.tile([P, S // 16], U16, name="offsets")
         nc.sync.dma_start(offsets[:], offs)

@@ -49,11 +49,12 @@ def tile_list_koopman_delay_lift_kernel(tc, xT, wgt, offs, w1, b1, wa_words, wa_
             nc.sync.dma_start(out=tile[:], in_=src)
             return tile
 
-        wgt_rows = load(
-            "wgt_rows",
-            [P, P],
-            wgt.rearrange("(n r) (u j) -> n r u j", r=S // P, j=P)[:, 0],
+        wgt_rows = at("wgt_rows", [P, P])
+        half_rows = wgt.rearrange("p (e c) -> (p e) c", c=W)
+        nc.sync.dma_start(
+            out=wgt_rows[0 : P // 2], in_=half_rows[0 : 2 * P : SHARE + 1].rearrange("n (u j) -> n u j", j=P)
         )
+        nc.vector.memset(wgt_rows[P // 2 : P], 0.0)
         offsets = keep.tile([P, S // 16], U16, name="offsets")
         nc.sync.dma_start(offsets[:], offs)
         identity = at("identity", [P, P])
@@ -76,10 +77,9 @@ def tile_list_koopman_delay_lift_kernel(tc, xT, wgt, offs, w1, b1, wa_words, wa_
             lo, hi = part_range(a, b, u)
             w1_part[a, b, u] = load("w1_%d_%d_%d" % (a, b, u), [P, PACK, hi - lo], w1_rows[a][:, :, b * W + lo : b * W + hi])
 
-        for n in range(6):
+        for n in range(7):
             load_x(n // PACK, n % PACK)
         load_w1(0, 0, 0)
-        load_x(1, 2)
         load_x(1, 3)
         load_w1(0, 0, 1)
         load_w1(1, 0, 0)
@@ -105,7 +105,7 @@ def tile_list_koopman_delay_lift_kernel(tc, xT, wgt, offs, w1, b1, wa_words, wa_
         def turn(n):
             turned = bank(n)
             nc.tensor.transpose(turned[:, 0:P], wgt_rows[:], identity[:])
-            return turned[:, 0:P].rearrange("j (g u) -> j u g", u=SHARE)
+            return turned[:, 0 : P // 2].rearrange("j (g u) -> j u g", g=HEADS)
 
         def spread_weight(copy, by_head, first, count, n):
             spread = at("spread_%d" % first, [P, count, HEADS, SHARE])

from contextlib import ExitStack

import concourse.mybir as mybir
from concourse.masks import make_identity

K, T, S, H, N = 1024, 2048, 1024, 1024, 512
FLOPS = 2 * K * H * S + 2 * 2 * H * N * S

F32 = mybir.dt.float32
BF16 = mybir.dt.bfloat16
I32 = mybir.dt.int32
U32 = mybir.dt.uint32
U16 = mybir.dt.uint16
U8 = mybir.dt.uint8
FP8X4 = mybir.dt.float8_e4m3fn_x4
FP4X4 = mybir.dt.float4_e2m1fn_x4
MULT = mybir.AluOpType.mult
ADD = mybir.AluOpType.add
IDENTITY = mybir.ActivationFunctionType.Identity
SQUARE = mybir.ActivationFunctionType.Square

P = 128
PACK = 4
PASSES = 2
W = 512
Q = W // 2
GROUPS = N // P
RUN = 4
HEADS = 8
SHARE = P // HEADS
EARLY = 3 * W // 4


def tile_list_koopman_delay_lift_kernel(tc, xT, wgt, offs, w1, b1, wa_words, wa_scales, wb, drive, out):
    nc = tc.nc
    with ExitStack() as ctx:
        keep = ctx.enter_context(tc.tile_pool(name="keep", bufs=1))
        psum = ctx.enter_context(tc.psum_pool(name="psum", bufs=1))
        on_vector, on_scalar = nc.vector.tensor_copy, nc.scalar.copy

        def bank(n):
            return psum.tile([P, W], F32, name="bank_%d" % n)

        def at(place, shape, dtype=F32):
            return keep.tile(shape, dtype, name=place, align_bytes=64)

        def load(place, shape, src):
            tile = at(place, shape)
            nc.sync.dma_start(out=tile[:], in_=src)
            return tile

        wgt_rows = at("wgt_rows", [P, P])
        half_rows = wgt.rearrange("p (e c) -> (p e) c", c=W)
        nc.sync.dma_start(
            out=wgt_rows[0 : P // 2], in_=half_rows[0 : 2 * P : SHARE + 1].rearrange("n (u j) -> n u j", j=P)
        )
        nc.vector.memset(wgt_rows[P // 2 : P], 0.0)
        offsets = keep.tile([P, S // 16], U16, name="offsets")
        nc.sync.dma_start(offsets[:], offs)
        identity = at("identity", [P, P])
        make_identity(nc, identity[:])
        wa_scale_rows = at("wa_scale_rows", [P, PASSES, N], U8)
        nc.gpsimd.memset(wa_scale_rows[:].bitcast(I32), 0)

        x_rows = xT.rearrange("(a p i) t -> a i p t", a=PASSES, i=PACK)
        w1_rows = w1.rearrange("(a p i) r -> a p i r", a=PASSES, i=PACK)
        x_plane, w1_part = {}, {}
        cuts = {(0, 0): (0, EARLY, W), (1, 0): (0, Q, EARLY, W), (0, 1): (0, Q, W), (1, 1): (0, EARLY, W)}

        def load_x(a, i):
            x_plane[a, i] = load("x_%d_%d" % (a, i), [P, T], x_rows[a, i])

        def part_range(a, b, u):
            return cuts[a, b][u : u + 2]

        def load_w1(a, b, u):
            lo, hi = part_range(a, b, u)
            w1_part[a, b, u] = load("w1_%d_%d_%d" % (a, b, u), [P, PACK, hi - lo], w1_rows[a][:, :, b * W + lo : b * W + hi])

        for n in range(7):
            load_x(n // PACK, n % PACK)
        load_w1(0, 0, 0)
        load_x(1, 3)
        load_w1(0, 0, 1)
        load_w1(1, 0, 0)
        load_w1(1, 0, 1)
        load_w1(1, 0, 2)
        bias = load("bias", [P, PASSES, PACK], b1.rearrange("(b p t) -> p b t", b=PASSES, t=PACK))
        load_w1(0, 1, 0)
        load_w1(0, 1, 1)
        load_w1(1, 1, 0)
        load_w1(1, 1, 1)
        wb_rows = wb.rearrange("(b p t) n -> b p t n", b=PASSES, t=PACK)
        wb_block = [load("wb_%d" % b, [P, PACK, W], wb_rows[b]) for b in range(PASSES)]
        wa_codes = at("wa_codes", [P, PASSES, 2 * N], U8)
        nc.sync.dma_start(out=wa_codes[:].bitcast(I32), in_=wa_words.rearrange("b p c -> p b c").bitcast(I32))
        for q in range(4):
            nc.sync.dma_start(
                out=wa_scale_rows[32 * q : 32 * q + 4].bitcast(I32),
                in_=wa_scales[:, 4 * q : 4 * q + 4, :].rearrange("b r n -> r b n").bitcast(I32),
            )

        weight = at("weight", [P, S])

        def turn(n):
            turned = bank(n)
            nc.tensor.transpose(turned[:, 0:P], wgt_rows[:], identity[:])
            return turned[:, 0 : P // 2].rearrange("j (g u) -> j u g", g=HEADS)

        def spread_weight(copy, by_head, first, count, n):
            spread = at("spread_%d" % first, [P, count, HEADS, SHARE])
            copy(out=spread[:], in_=by_head[:, first : first + count, :].unsqueeze(3).to_broadcast([P, count, HEADS, SHARE]))
            back = bank(n)
            for c in range(count):
                nc.tensor.transpose(back[:, c * P : (c + 1) * P], spread[:, c].rearrange("j g s -> j (g s)"), identity[:])
            copy(out=weight[:, first * P : (first + count) * P], in_=back[:, 0 : count * P])

        for_vector, for_scalar = turn(0), turn(1)
        spread_weight(on_vector, for_vector, 0, 2, 2)
        spread_weight(on_scalar, for_scalar, 2, 2, 3)
        spread_weight(on_scalar, for_scalar, 4, 4, 4)

        def woven_tile(place, width=W):
            return at(place, [P, width, PACK], BF16)

        def weave(copy, src, place):
            dst = woven_tile(place)
            copy(
                out=dst[:].rearrange("p (c u) (s e) -> p c s u e", u=RUN, e=2),
                in_=src.rearrange("p (s e) (c u) -> p c s u e", u=RUN, e=2),
            )
            return dst

        def weave_pair(copy, dst, src, first):
            copy(out=dst[:, :, first : first + 2], in_=src[:, first : first + 2, :].rearrange("p e j -> p j e"))

        def weave_w1(copy, dst, a, b, u):
            lo, hi = part_range(a, b, u)
            copy(
                out=dst[:].rearrange("p (t m) (s e) -> p m s t e", t=PACK, e=2)[:, lo // PACK : hi // PACK],
                in_=w1_part[a, b, u][:].rearrange("p (s e) (m t) -> p m s t e", t=PACK, e=2),
            )

        def weave_square(z, place, width=W):
            dst = woven_tile(place, width)
            nc.scalar.activation(
                out=dst[:].rearrange("p (c u) t -> p c t u", u=RUN), in_=z.rearrange("p t (c u) -> p c t u", u=RUN), func=SQUARE
            )
            return dst

        def quantise(src, name, width=W, place=None):
            codes = at(place or name + "_codes", [P, width], U32)
            scales = at(name + "_scales", [P, width], U8)
            nc.vector.quantize_mx(out=codes[:].bitcast(FP8X4), scales=scales[:], in_=src[:].rearrange("p c t -> p (c t)"))
            return codes, scales

        picked = [at("picked_%d" % a, [P, PACK, S]) for a in range(PASSES)]

        def gather(a, i, lo=0, hi=S):
            window = x_plane[a, i][:].indirect(offsets[:, lo // 16 : hi // 16])
            nc.vector.tensor_tensor(picked[a][:, i, lo:hi], window, weight[:, lo:hi], MULT)

        def half(a, h):
            return picked[a][:, :, h * W : (h + 1) * W]

        def mx_pass(y, left, left_scales, right, start, stop):
            nc.tensor.matmul_mx(
                out=y, lhsT=left, lhsT_scale=left_scales, rhs=right[0].bitcast(FP8X4), rhs_scale=right[1], start=start, stop=stop
            )

        def part(q, lo, hi):
            return q[0][:, lo:hi], q[1][:, lo:hi]

        xq, w1q, wbq, zq, sq = {}, {}, {}, {}, {}

        def lift_pass(banks, a, b, h, t, first):
            codes, scales = part(w1q[a, b], t * P, (t + 1) * P)
            mx_pass(banks[t][:], codes.bitcast(FP8X4), scales, part(xq[a, h], 0, W), a == first, a != first)

        def lift(b, h, side, place, opened, first):
            banks = [bank(PACK * side + t) for t in range(PACK)]
            for t in range(opened):
                lift_pass(banks, first, b, h, t, first)
            return banks, b, h, place, opened, first

        def close(banks, b, h, place, opened, first):
            z = at(place, [P, PACK, W])
            for t in range(PACK):
                if t < opened:
                    lift_pass(banks, 1 - first, b, h, t, first)
                else:
                    lift_pass(banks, 1 - first, b, h, t, 1 - first)
                    lift_pass(banks, first, b, h, t, 1 - first)
                nc.scalar.activation(out=z[:, t, :], in_=banks[t][:], func=IDENTITY, bias=bias[:, b, t : t + 1])
            return z

        def linear_pass(y, b, g, z, start):
            left = wa_codes[:, b, 2 * g * P : 2 * (g + 1) * P].bitcast(FP4X4)
            mx_pass(y, left, wa_scale_rows[:, b, g * P : (g + 1) * P], z, start, False)

        def quadratic_pass(y, b, g, s, stop):
            codes, scales = part(wbq[b], g * P, (g + 1) * P)
            mx_pass(y, codes.bitcast(FP8X4), scales, s, False, stop)

        x01 = woven_tile("s_ring_1")
        gather(0, 0, 0, W)
        gather(0, 0, W, S)
        gather(0, 1)
        weave_pair(on_scalar, x01, half(0, 1), 0)
        gather(0, 2)
        gather(0, 3)
        x00 = weave(on_scalar, half(0, 0), "s_ring_0")
        weave_pair(on_scalar, x01, half(0, 1), 2)
        gather(1, 0)
        xq[0, 0] = quantise(x00, "xq00")
        gather(1, 1)
        w00 = woven_tile("s_ring_2")
        weave_w1(on_scalar, w00, 0, 0, 0)
        x10 = woven_tile("w1_0_0_0")
        weave_pair(on_scalar, x10, half(1, 0), 0)
        gather(1, 2)
        weave_w1(on_scalar, w00, 0, 0, 1)
        gather(1, 3, 0, W)
        gather(1, 3, W, S)
        weave_pair(on_vector, x10, half(1, 0), 2)
        w10 = woven_tile("s_ring_0")
        weave_w1(on_scalar, w10, 1, 0, 0)
        weave_w1(on_scalar, w10, 1, 0, 1)
        weave_w1(on_scalar, w10, 1, 0, 2)
        x11 = weave(on_scalar, half(1, 1), "w1_1_0_2")
        w1q[0, 0] = quantise(w00, "w1q00", place="x_1_3")
        unit00 = lift(0, 0, 0, "picked_0", 2, 0)
        xq[1, 0] = quantise(x10, "xq10")
        w1q[1, 0] = quantise(w10, "w1q10", place="x_0_2")
        z00 = close(*unit00)

        xq[0, 1] = quantise(x01, "xq01", place="w1_1_0_0")
        w01 = woven_tile("v_ring_1")
        weave_w1(on_vector, w01, 0, 1, 0)
        weave_w1(on_vector, w01, 0, 1, 1)
        xq[1, 1] = quantise(x11, "xq11")
        unit01 = lift(0, 1, 1, "x_0_1", 0, 0)
        w1q[0, 1] = quantise(w01, "w1q01")
        s00 = weave_square(z00[:], "x_0_0")
        z01 = close(*unit01)
        unit10 = lift(1, 0, 0, "x_1_2", PACK, 0)
        w11 = woven_tile("v_ring_0")
        weave_w1(on_vector, w11, 1, 1, 0)
        weave_w1(on_vector, w11, 1, 1, 1)
        z00w = weave(on_vector, z00[:], "x_1_1")
        w1q[1, 1] = quantise(w11, "w1q11")
        z10 = close(*unit10)
        s10 = weave_square(z10[:], "s_ring_3")
        zq[0, 0] = quantise(z00w, "zq00")
        wb0 = weave(on_vector, wb_block[0][:], "v_ring_1")
        sq[0, 0] = quantise(s00, "sq00")
        z01w = weave(on_vector, z01[:], "v_ring_0")
        wbq[0] = quantise(wb0, "wbq0")
        wb1 = weave(on_vector, wb_block[1][:], "s_ring_1")
        z10w = weave(on_vector, z10[:], "wb_0")
        wbq[1] = quantise(wb1, "wbq1")
        zq[1, 0] = quantise(z10w, "zq10")
        sq[1, 0] = quantise(s10, "sq10")
        zq[0, 1] = quantise(z01w, "zq01")

        drive_rows = drive.rearrange("(g p) j -> p g j", p=P)
        out_rows = out.rearrange("(g p) j -> p g j", p=P)
        given = [load(("x_1_0", "x_1_3")[h], [P, GROUPS, W], drive_rows[:, :, h * W : (h + 1) * W]) for h in range(2)]

        y0 = [bank(PACK + g) for g in range(GROUPS)]
        for g in range(GROUPS):
            linear_pass(y0[g][:], 0, g, part(zq[0, 0], 0, W), True)
        for g in range(GROUPS):
            quadratic_pass(y0[g][:], 0, g, part(sq[0, 0], 0, W), False)
        z11 = close(*lift(1, 1, 0, "x_0_3", PACK, 0))
        for g in range(GROUPS):
            linear_pass(y0[g][:], 1, g, part(zq[1, 0], 0, W), False)
        for g in range(GROUPS):
            quadratic_pass(y0[g][:], 1, g, part(sq[1, 0], 0, W), True)

        def finish_half0(g):
            nc.vector.tensor_tensor(given[0][:, g, :], y0[g][:], given[0][:, g, :], ADD)
            nc.sync.dma_start(out=out_rows[:, g, 0:W], in_=given[0][:, g, :])

        y1 = [[bank(2 * u + v) for v in range(2)] for u in range(2)]

        def y1_view(u, g):
            return y1[u][g // 2][:, (g % 2) * Q : (g % 2 + 1) * Q]

        def linear_quarter(b, u):
            for g in range(GROUPS):
                linear_pass(y1_view(u, g), b, g, part(zq[b, 1], u * Q, (u + 1) * Q), b == 0 and g % 2 == 0)

        def quadratic_quarter(b, u, woven):
            codes = quantise(woven, "sq%d1_%d" % (b, u), Q)
            for g in range(GROUPS):
                quadratic_pass(y1_view(u, g), b, g, part(codes, 0, Q), b == 1 and g % 2 == 1)

        def finish_quarter(u, v):
            rows = at(("wb_1", "x_1_2", "picked_0", "picked_1")[2 * u + v], [P, 2, Q])
            nc.vector.tensor_tensor(
                rows[:], y1[u][v][:].rearrange("p (g j) -> p g j", g=2), given[1][:, 2 * v : 2 * v + 2, u * Q : (u + 1) * Q], ADD
            )
            nc.sync.dma_start(out=out_rows[:, 2 * v : 2 * v + 2, W + u * Q : W + (u + 1) * Q], in_=rows[:])

        def square_quarter(b, u):
            place = (("w1q11_codes", "s_ring_2"), ("xq11_codes", "v_ring_1"))[u][b]
            return weave_square((z01, z11)[b][:, :, u * Q : (u + 1) * Q], place, Q)

        squares = {(b, u): square_quarter(b, u) for u in range(2) for b in range(PASSES)}
        finish_half0(0)
        linear_quarter(0, 0)
        linear_quarter(0, 1)
        z11w = weave(on_vector, z11[:], "s_ring_0")
        quadratic_quarter(0, 0, squares[0, 0])
        zq[1, 1] = quantise(z11w, "zq11")
        linear_quarter(1, 0)
        quadratic_quarter(1, 0, squares[1, 0])
        linear_quarter(1, 1)
        finish_half0(1)
        quadratic_quarter(0, 1, squares[0, 1])
        finish_half0(2)
        finish_half0(3)
        finish_quarter(0, 0)
        quadratic_quarter(1, 1, squares[1, 1])
        finish_quarter(0, 1)
        finish_quarter(1, 0)
        finish_quarter(1, 1)
